import numpy as np
import ml_dtypes


def mxq(x, axis, fmt="e4m3"):
    dtype, down = {"e4m3": (ml_dtypes.float8_e4m3fn, 7), "e5m2": (ml_dtypes.float8_e5m2, 14)}[fmt]
    v = np.moveaxis(np.asarray(x, np.float32).astype(ml_dtypes.bfloat16).astype(np.float64), axis, -1)
    blocks = v.reshape(v.shape[:-1] + (-1, 32))
    amax = np.abs(blocks).max(-1, keepdims=True)
    byte = np.maximum(np.where(amax > 0, np.frexp(amax)[1] - 1 + 127, 0) - down, 1)
    scale = np.exp2(byte - 127.0)
    codes = (blocks / scale).astype(np.float32).astype(dtype).astype(np.float64)
    return np.moveaxis((codes * scale).reshape(v.shape), -1, axis)


WIDE = False


def mx_kscale(k):
    if not WIDE:
        return np.ones(k)
    levels = np.array([10, -10, 5, -5, 0])
    if k % 512:
        return np.exp2(np.random.permutation(np.resize(levels, k // 32))).repeat(32)
    a = np.empty((k // 512, 16))
    for p in range(k // 512):
        a[p, :8] = np.random.permutation(np.resize(levels, 8))
        for g in range(8):
            far = levels[np.abs(levels - a[p, g]) >= 10]
            a[p, g + 8] = far[np.random.randint(len(far))]
    return np.exp2(a.ravel()).repeat(32)


def f64(x):
    return np.asarray(x).astype(np.float64)


def striped(idx):
    return np.tile(idx.reshape(-1, 16).T, (8, 1)).astype(np.uint16)


def unstriped(offs):
    return offs[:16].T.reshape(-1).astype(np.int64)


def striped8(idx):
    return np.concatenate([x.reshape(-1, 16).T for x in idx]).astype(np.uint16)


def runs(offs, k):
    lists = np.stack([offs[16 * r : 16 * r + 16].T.reshape(-1) for r in range(8)]).astype(np.int64)
    return lists[np.arange(k) % 512 // 64]


def pack_weight(w):
    k, n = w.shape
    w = f64(np.asarray(w, np.float32).astype(ml_dtypes.bfloat16)).reshape(k // 32, 32, n)
    amax = np.abs(w).max(1)
    byte = np.clip(np.where(amax > 0, np.frexp(amax)[1] - 1 + 127 - 7, 1), 1, 254)
    scaled = (w * np.exp2(127.0 - byte)[:, None, :]).reshape(k, n).astype(np.float32)
    words = np.ascontiguousarray(scaled.reshape(k // 512, 128, 4, n).transpose(0, 1, 3, 2)).astype(ml_dtypes.float8_e4m3fn).view(np.uint8)
    return words, np.ascontiguousarray(byte.astype(np.uint8).reshape(k // 512, 16, n))


def unpack_weight(words, scales):
    g, p, n, _ = words.shape
    vals = np.ascontiguousarray(words).view(ml_dtypes.float8_e4m3fn).astype(np.float64) * np.repeat(np.exp2(scales.astype(np.float64) - 127.0), 8, axis=1)[..., None]
    return vals.transpose(0, 1, 3, 2).reshape(g * 512, n)


E2M1 = np.array([0.0, 0.5, 1.0, 1.5, 2.0, 3.0, 4.0, 6.0, -0.0, -0.5, -1.0, -1.5, -2.0, -3.0, -4.0, -6.0])


def pack_fp4(w):
    k, n = w.shape
    w = f64(np.asarray(w, np.float32).astype(ml_dtypes.bfloat16)).reshape(k // 32, 32, n)
    amax = np.abs(w).max(1)
    mant, ex = np.frexp(amax / 6.0)
    byte = np.clip(np.where(amax > 0, np.where(mant > 0.5, ex, ex - 1) + 127, 1), 1, 254)
    scaled = (w * np.exp2(127.0 - byte)[:, None, :]).reshape(k, n).astype(np.float32)
    c = np.ascontiguousarray(scaled.reshape(k // 512, 128, 4, n).transpose(0, 1, 3, 2)).astype(ml_dtypes.float4_e2m1fn).view(np.uint8) & 0xF
    words = (c[..., 0::2] | (c[..., 1::2] << 4)).reshape(k // 512, 128, 2 * n)
    return np.ascontiguousarray(words), np.ascontiguousarray(byte.astype(np.uint8).reshape(k // 512, 16, n))


def unpack_fp4(words, scales):
    g, _, n = scales.shape
    words = np.ascontiguousarray(words).reshape(g, 128, n, 2)
    nib = np.empty((g, 128, n, 4), np.uint8)
    nib[..., 0::2] = words & 0xF
    nib[..., 1::2] = words >> 4
    vals = E2M1[nib] * np.repeat(np.exp2(scales.astype(np.float64) - 127.0), 8, axis=1)[..., None]
    return vals.transpose(0, 1, 3, 2).reshape(g * 512, n)


def sigmoid(v):
    return 1.0 / (1.0 + np.exp(-np.maximum(v, -700.0)))

def planes(y):
    n, m = y.shape
    v = y.astype(np.float32).astype(ml_dtypes.bfloat16).astype(np.float64).reshape(n // 32, 32, m)
    top = np.abs(v).max(1)
    byte = np.clip(np.where(top > 0, np.frexp(top)[1] - 1 + 127 - 7, 1), 1, 254)
    codes = (v * np.exp2(127.0 - byte)[:, None, :]).reshape(n, m).astype(np.float32).astype(ml_dtypes.float8_e4m3fn).view(np.uint8)
    words = codes.reshape(n // 512, 128, 4, m).transpose(0, 1, 3, 2)
    return np.ascontiguousarray(words), np.ascontiguousarray(byte.astype(np.uint8).reshape(n // 512, 16, m))


K, T, S, N, H, W, U = 512, 2048, 512, 512, 512, 256, 1024


def setup_inputs():
    n = np.random.standard_normal
    s = mx_kscale(K)[:, None]
    u = mx_kscale(H)
    packed_xT = pack_weight(n((K, T)) * s)
    packed_w1 = pack_fp4(n((K, H)) / np.sqrt(K) / s)
    packed_w2 = pack_fp4(n((K, H)) / np.sqrt(K) / s)
    packed_w3 = pack_fp4(n((K, H)) / np.sqrt(K) / s)
    packed_w4 = pack_fp4(n((H, N)) / np.sqrt(H) / u[:, None])
    return {
        "x_words": packed_xT[0],
        "x_scales": packed_xT[1],
        "w1_words": packed_w1[0],
        "w1_scales": packed_w1[1],
        "w2_words": packed_w2[0],
        "w2_scales": packed_w2[1],
        "w3_words": packed_w3[0],
        "w3_scales": packed_w3[1],
        "gn": (np.random.uniform(0.5, 1.5, (H, 1)) * u[:, None]).astype(np.float32),
        "w4_words": packed_w4[0],
        "w4_scales": packed_w4[1],
        "mem": n((N, U)).astype(np.float32),
        "offs": striped(np.random.permutation(T)[:S]),
        "two": striped(np.random.permutation(T)[:S]),
        "three": striped(np.random.permutation(T)[:S]),
        "n1": striped8(np.stack([np.random.permutation(S) for _ in range(8)])),
        "n2": striped8(np.stack([np.random.permutation(S) for _ in range(8)])),
        "n3": striped8(np.stack([np.random.permutation(S)[:W] for _ in range(8)])),
        "n4": striped8(np.stack([np.random.permutation(S)[:W] for _ in range(8)])),
        "n5": striped8(np.stack([np.random.permutation(U)[:S] for _ in range(8)])),
    }


def reference(x_words, x_scales, w1_words, w1_scales, w2_words, w2_scales, w3_words, w3_scales, gn, w4_words, w4_scales, mem, offs, two, three, n1, n2, n3, n4, n5):
    x_three = unpack_weight(x_words, x_scales)[:, unstriped(three)]
    b = unpack_fp4(w3_words, w3_scales).T @ x_three
    xq = unpack_weight(x_words, x_scales)[:, unstriped(offs)]
    y = unpack_fp4(w1_words, w1_scales).T @ xq
    x_two = unpack_weight(x_words, x_scales)[:, unstriped(two)]
    d = unpack_fp4(w2_words, w2_scales).T @ x_two
    m1 = y + (sigmoid(d[np.arange(H)[:, None], runs(n2, H)] - d)) * (y[np.arange(H)[:, None], runs(n1, H)] - y)
    ra = b[np.arange(H)[:, None], runs(n4, H)] - (0.5 * (m1[np.arange(H)[:, None], runs(n3, H)]))
    ds = m1.copy()
    ds[np.arange(H)[:, None], runs(n3, H)] = ra
    z = f64(gn) * ds
    h = unpack_fp4(w4_words, w4_scales).T @ mxq(z, 0, "e4m3")
    nw = np.maximum(h, 0.5 * (f64(mem)[np.arange(N)[:, None], runs(n5, N)]))
    out = f64(mem).copy()
    out[np.arange(N)[:, None], runs(n5, N)] = nw
    return (out,) + planes(out)

@@ -1,0 +1,259 @@
+from contextlib import ExitStack
+
+import concourse.mybir as mybir
+
+K, T, S, N, H, W, U = 512, 2048, 512, 512, 512, 256, 1024
+FLOPS = 4 * 2 * 512 * 512 * 512
+
+F32 = mybir.dt.float32
+BF16 = mybir.dt.bfloat16
+I32 = mybir.dt.int32
+U32 = mybir.dt.uint32
+U16 = mybir.dt.uint16
+U8 = mybir.dt.uint8
+FP8X4 = mybir.dt.float8_e4m3fn_x4
+FP4X4 = mybir.dt.float4_e2m1fn_x4
+ALU = mybir.AluOpType
+ACT = mybir.ActivationFunctionType
+
+P = 128
+PACK = 4
+QUADS = 4
+CHUNKS = ((0, 512), (512, 256), (768, 256))
+
+
+def tile_picked_triopullbputbpagex_none_po_kernel(
+    tc, x_words, x_scales, w1_words, w1_scales, w2_words, w2_scales, w3_words, w3_scales, gn,
+    w4_words, w4_scales, mem, offs, two, three, n1, n2, n3, n4, n5, out_0, out_1, out_2,
+):
+    nc = tc.nc
+    with ExitStack() as ctx:
+        keep = ctx.enter_context(tc.tile_pool(name="keep", bufs=1))
+        psum = ctx.enter_context(tc.psum_pool(name="psum", bufs=8))
+
+        def sb(name, shape, dtype, tag=None):
+            return keep.tile(shape, dtype, name=name, tag=tag or name, align_bytes=64)
+
+        def load_list(name, src):
+            lst = keep.tile(list(src.shape), U16, name=name)
+            nc.sync.dma_start(lst[:], src)
+            return lst
+
+        def scale_tile(name, width, engine):
+            rows = sb(name, [P, width], U8)
+            engine.memset(rows[:].bitcast(I32), 0)
+            return rows
+
+        def load_scale_rows(rows, src):
+            for q in range(QUADS):
+                nc.sync.dma_start(rows[32 * q : 32 * q + 4, :].bitcast(I32), src[0, 4 * q : 4 * q + 4, :].bitcast(I32))
+
+        def load_words(name, src):
+            raw = sb(name, [P, 2 * H], U8)
+            nc.sync.dma_start(raw[:].bitcast(I32), src[0].bitcast(I32))
+            return raw
+
+        def deal_words(name, raw):
+            dealt = sb(name, [P, 2 * H], U8)
+            nc.vector.tensor_copy(
+                out=dealt[:].rearrange("p (t m b) -> p t m b", t=PACK, b=2),
+                in_=raw[:].rearrange("p (m t b) -> p t m b", t=PACK, b=2),
+            )
+            return dealt
+
+        def deal_scales(name, raw):
+            dealt = sb(name, [P, H], U8)
+            nc.vector.tensor_copy(
+                out=dealt[:].rearrange("p (t m) -> p t m", t=PACK),
+                in_=raw[:].rearrange("p (m t) -> p t m", t=PACK),
+            )
+            return dealt
+
+        def pick(name, table, lst, dtype):
+            picked = sb(name, [P, S], dtype)
+            nc.vector.tensor_copy(picked[:], table[:].indirect(lst[:]))
+            return picked
+
+        def product(name, w_codes, w_planes, t, codes, planes):
+            acc = psum.tile([P, S], F32, name=name, tag="acc")
+            nc.tensor.matmul_mx(
+                out=acc[:],
+                lhsT=w_codes[:, 2 * P * t : 2 * P * (t + 1)].bitcast(FP4X4),
+                lhsT_scale=w_planes[:, P * t : P * (t + 1)],
+                rhs=codes[:].bitcast(FP8X4),
+                rhs_scale=planes[:],
+                start=True,
+                stop=True,
+            )
+            return acc
+
+        xs = scale_tile("xs", T, nc.vector)
+        w2s_raw = scale_tile("w2s_raw", H, nc.gpsimd)
+        w1s_raw = scale_tile("w1s_raw", H, nc.gpsimd)
+        w3s_raw = scale_tile("w3s_raw", H, nc.gpsimd)
+        w4s_raw = scale_tile("w4s_raw", N, nc.gpsimd)
+        warm = sb("warm", [P, 1], F32)
+        warm2 = sb("warm2", [P, 1], F32)
+        nc.gpsimd.memset(warm[:], 0.0)
+        nc.scalar.activation(warm2[:], warm[:], ACT.Sigmoid)
+
+        l_two = load_list("l_two", two)
+        w2_raw = load_words("w2_raw", w2_words)
+        w1_raw = load_words("w1_raw", w1_words)
+        load_scale_rows(xs, x_scales)
+        xw = sb("xw", [P, T], U32)
+        nc.sync.dma_start(xw[:].bitcast(I32), x_words[0].rearrange("p n t -> p (n t)").bitcast(I32))
+        l_offs = load_list("l_offs", offs)
+        load_scale_rows(w2s_raw, w2_scales)
+        l_three = load_list("l_three", three)
+        load_scale_rows(w1s_raw, w1_scales)
+        w3_raw = load_words("w3_raw", w3_words)
+        l_n2 = load_list("l_n2", n2)
+        l_n1 = load_list("l_n1", n1)
+        load_scale_rows(w3s_raw, w3_scales)
+        l_n4 = load_list("l_n4", n4)
+        l_n3 = load_list("l_n3", n3)
+        gain = sb("gain", [P, PACK], F32)
+        nc.sync.dma_start(gain[:], gn.rearrange("(p t) o -> p (t o)", t=PACK))
+        l_n5 = load_list("l_n5", n5)
+        w4_raw = load_words("w4_raw", w4_words)
+        load_scale_rows(w4s_raw, w4_scales)
+        mem_rows = mem.rearrange("(p t) u -> p t u", t=PACK)
+        out_rows = out_0.rearrange("(p t) u -> p t u", t=PACK)
+        page = []
+        for t in range(PACK):
+            page.append(sb("page%d" % t, [P, U], F32))
+            nc.sync.dma_start(page[t][:], mem_rows[:, t, :])
+
+        w2c = deal_words("w2c", w2_raw)
+        w1c = deal_words("w1c", w1_raw)
+        s_two = pick("s_two", xs, l_two, U8)
+        s_offs = pick("s_offs", xs, l_offs, U8)
+        c_two = pick("c_two", xw, l_two, U32)
+        w2p = deal_scales("w2p", w2s_raw)
+        c_offs = pick("c_offs", xw, l_offs, U32)
+        w1p = deal_scales("w1p", w1s_raw)
+        s_three = pick("s_three", xs, l_three, U8)
+        c_three = pick("c_three", xw, l_three, U32)
+        w3c = deal_words("w3c", w3_raw)
+        w3p = deal_scales("w3p", w3s_raw)
+
+        dwin, ywin, bwin, u, sg, e, bg, pr, m1, ds, mg = ({} for i in range(11))
+        z = sb("z", [P, S, PACK], BF16)
+
+        def project(t):
+            dwin[t] = sb("dwin%d" % t, [P, 2 * S], F32)
+            ywin[t] = sb("ywin%d" % t, [P, 2 * S], F32)
+            bwin[t] = sb("bwin%d" % t, [P, S], F32)
+            d_ps = product("d_ps", w2c, w2p, t, c_two, s_two)
+            y_ps = product("y_ps", w1c, w1p, t, c_offs, s_offs)
+            b_ps = product("b_ps", w3c, w3p, t, c_three, s_three)
+            nc.scalar.copy(dwin[t][:, :S], d_ps[:])
+            nc.scalar.copy(ywin[t][:, S:], d_ps[:])
+            nc.scalar.copy(dwin[t][:, S:], y_ps[:])
+            nc.scalar.copy(ywin[t][:, :S], y_ps[:])
+            nc.scalar.copy(bwin[t][:], b_ps[:])
+
+        def gate(t):
+            u[t] = sb("u%d" % t, [P, S], F32)
+            sg[t] = sb("sg%d" % t, [P, S], F32)
+            nc.vector.tensor_tensor(u[t][:], dwin[t][:].indirect(l_n2[:]), ywin[t][:, S:], ALU.subtract)
+            nc.scalar.activation(sg[t][:], u[t][:], ACT.Sigmoid)
+
+        def pull(t):
+            e[t] = sb("e%d" % t, [P, S], F32)
+            nc.vector.tensor_tensor(e[t][:], ywin[t][:].indirect(l_n1[:]), dwin[t][:, S:], ALU.subtract)
+
+        def fetch_b(t):
+            bg[t] = sb("bg%d" % t, [P, W], F32)
+            nc.vector.tensor_copy(bg[t][:], bwin[t][:].indirect(l_n4[:]))
+
+        def gated(t):
+            pr[t] = sb("pr%d" % t, [P, S], F32)
+            nc.vector.tensor_tensor(pr[t][:], sg[t][:], e[t][:], ALU.mult)
+
+        def mix(t):
+            m1[t] = sb("m1_%d" % t, [P, S], F32)
+            ds[t] = sb("ds%d" % t, [P, S], F32)
+            nc.vector.tensor_tensor(m1[t][:], pr[t][:], dwin[t][:, S:], ALU.add)
+            nc.scalar.copy(ds[t][:], m1[t][:])
+
+        def fetch_m(t):
+            mg[t] = sb("mg%d" % t, [P, W], F32)
+            nc.vector.tensor_scalar(mg[t][:], m1[t][:].indirect(l_n3[:]), -0.5, 0.0, ALU.mult, ALU.add)
+
+        def put(t):
+            nc.vector.tensor_tensor(ds[t][:].indirect(l_n3[:]), bg[t][:], mg[t][:], ALU.add)
+            nc.scalar.activation(z[:, :, t], ds[t][:], ACT.Copy, scale=gain[:, t : t + 1])
+
+        half = {}
+
+        def fetch_page(t, tag):
+            half[t] = sb("half%d" % t, [P, S], F32, tag=tag)
+            nc.vector.tensor_scalar(half[t][:], page[t][:].indirect(l_n5[:]), 0.5, 0.0, ALU.mult, ALU.add)
+
+        last = PACK - 1
+        project(0)
+        project(1)
+        gate(0)
+        pull(0)
+        fetch_b(0)
+        for t in range(PACK):
+            gated(t)
+            if t + 2 < PACK:
+                project(t + 2)
+            if t < last:
+                gate(t + 1)
+            else:
+                w4c = deal_words("w4c", w4_raw)
+            mix(t)
+            if t < last:
+                pull(t + 1)
+            else:
+                w4p = deal_scales("w4p", w4s_raw)
+            fetch_m(t)
+            if t < last:
+                fetch_b(t + 1)
+            else:
+                fetch_page(0, "pr%d" % last)
+            put(t)
+
+        fetch_page(1, "bg%d" % last)
+        fetch_page(2, "mg%d" % last)
+        z_codes = sb("z_codes", [P, S], U32)
+        z_planes = sb("z_planes", [P, S], U8)
+        nc.vector.quantize_mx(out=z_codes[:].bitcast(FP8X4), scales=z_planes[:], in_=z[:].rearrange("p c t -> p (c t)"))
+        fetch_page(3, "z")
+
+        woven = [sb("woven%d" % i, [P, n, PACK], BF16) for i, (c0, n) in enumerate(CHUNKS)]
+        h_ps = [product("h_ps", w4c, w4p, t, z_codes, z_planes) for t in range(PACK)]
+        nw = {}
+
+        def larger(t):
+            nw[t] = sb("nw%d" % t, [P, S], F32)
+            nc.vector.tensor_tensor(nw[t][:], h_ps[t][:], half[t][:], ALU.max)
+
+        larger(0)
+        for t in range(PACK):
+            if t < last:
+                larger(t + 1)
+            nc.vector.tensor_copy(page[t][:].indirect(l_n5[:]), nw[t][:])
+            nc.sync.dma_start(out_rows[:, t, :], page[t][:])
+            for i, (c0, n) in enumerate(CHUNKS):
+                if t == last and i == 0:
+                    nc.vector.tensor_copy(woven[i][:, :, t], page[t][:, c0 : c0 + n])
+                elif t == last - 1 and i == 0:
+                    nc.scalar.copy(woven[i][:, :, t:], page[t][:, c0 : c0 + n].unsqueeze(2).to_broadcast([P, n, 2]))
+                else:
+                    nc.scalar.copy(woven[i][:, :, t], page[t][:, c0 : c0 + n])
+
+        o_planes = sb("o_planes", [P, U], U8)
+        words_out = out_1[0].rearrange("p n t -> p (n t)").bitcast(I32)
+        for i, (c0, n) in enumerate(CHUNKS):
+            o_codes = sb("o_codes%d" % i, [P, n], U32)
+            nc.vector.quantize_mx(
+                out=o_codes[:].bitcast(FP8X4), scales=o_planes[:, c0 : c0 + n], in_=woven[i][:].rearrange("p c t -> p (c t)")
+            )
+            nc.sync.dma_start(words_out[:, c0 : c0 + n], o_codes[:].bitcast(I32))
+        for q in range(QUADS):
+            nc.sync.dma_start(out_2[0, 4 * q : 4 * q + 4, :].bitcast(I32), o_planes[32 * q : 32 * q + 4, :].bitcast(I32))

@@ -1,6 +1,7 @@
 from contextlib import ExitStack
 
 import concourse.mybir as mybir
+from concourse.masks import make_identity
 
 K, T, S, N, H, W, U = 512, 2048, 512, 512, 512, 256, 1024
 FLOPS = 4 * 2 * 512 * 512 * 512
@@ -29,7 +30,7 @@ def tile_picked_triopullbputbpagex_none_po_kernel(
     nc = tc.nc
     with ExitStack() as ctx:
         keep = ctx.enter_context(tc.tile_pool(name="keep", bufs=1))
-        psum = ctx.enter_context(tc.psum_pool(name="psum", bufs=8))
+        psum = ctx.enter_context(tc.psum_pool(name="psum", bufs=1))
 
         def sb(name, shape, dtype, tag=None):
             return keep.tile(shape, dtype, name=name, tag=tag or name, align_bytes=64)
@@ -74,8 +75,8 @@ def tile_picked_triopullbputbpagex_none_po_kernel(
             nc.vector.tensor_copy(picked[:], table[:].indirect(lst[:]))
             return picked
 
-        def product(name, w_codes, w_planes, t, codes, planes):
-            acc = psum.tile([P, S], F32, name=name, tag="acc")
+        def product(name, w_codes, w_planes, t, codes, planes, tag="acc"):
+            acc = psum.tile([P, S], F32, name=name, tag=tag, bufs=2)
             nc.tensor.matmul_mx(
                 out=acc[:],
                 lhsT=w_codes[:, 2 * P * t : 2 * P * (t + 1)].bitcast(FP4X4),
@@ -87,7 +88,7 @@ def tile_picked_triopullbputbpagex_none_po_kernel(
             )
             return acc
 
-        xs = scale_tile("xs", T, nc.vector)
+        xs = scale_tile("xs", T, nc.gpsimd)
         w2s_raw = scale_tile("w2s_raw", H, nc.gpsimd)
         w1s_raw = scale_tile("w1s_raw", H, nc.gpsimd)
         w3s_raw = scale_tile("w3s_raw", H, nc.gpsimd)
@@ -95,15 +96,17 @@ def tile_picked_triopullbputbpagex_none_po_kernel(
         warm = sb("warm", [P, 1], F32)
         warm2 = sb("warm2", [P, 1], F32)
         nc.gpsimd.memset(warm[:], 0.0)
+        ident = sb("ident", [P, P], F32)
+        make_identity(nc, ident[:])
         nc.scalar.activation(warm2[:], warm[:], ACT.Sigmoid)
 
+        load_scale_rows(xs, x_scales)
         l_two = load_list("l_two", two)
         w2_raw = load_words("w2_raw", w2_words)
-        w1_raw = load_words("w1_raw", w1_words)
-        load_scale_rows(xs, x_scales)
+        l_offs = load_list("l_offs", offs)
         xw = sb("xw", [P, T], U32)
         nc.sync.dma_start(xw[:].bitcast(I32), x_words[0].rearrange("p n t -> p (n t)").bitcast(I32))
-        l_offs = load_list("l_offs", offs)
+        w1_raw = load_words("w1_raw", w1_words)
         load_scale_rows(w2s_raw, w2_scales)
         l_three = load_list("l_three", three)
         load_scale_rows(w1s_raw, w1_scales)
@@ -125,64 +128,69 @@ def tile_picked_triopullbputbpagex_none_po_kernel(
             page.append(sb("page%d" % t, [P, U], F32))
             nc.sync.dma_start(page[t][:], mem_rows[:, t, :])
 
-        w2c = deal_words("w2c", w2_raw)
-        w1c = deal_words("w1c", w1_raw)
         s_two = pick("s_two", xs, l_two, U8)
+        w2c = deal_words("w2c", w2_raw)
         s_offs = pick("s_offs", xs, l_offs, U8)
         c_two = pick("c_two", xw, l_two, U32)
         w2p = deal_scales("w2p", w2s_raw)
         c_offs = pick("c_offs", xw, l_offs, U32)
+        w1c = deal_words("w1c", w1_raw)
         w1p = deal_scales("w1p", w1s_raw)
         s_three = pick("s_three", xs, l_three, U8)
         c_three = pick("c_three", xw, l_three, U32)
         w3c = deal_words("w3c", w3_raw)
         w3p = deal_scales("w3p", w3s_raw)
 
-        dwin, ywin, bwin, u, sg, e, bg, pr, m1, ds, mg = ({} for i in range(11))
+        dwin, ywin, bwin, y_t, dg, yg, s_t, e_t, bg, p_t, ds, mg = ({} for i in range(12))
         z = sb("z", [P, S, PACK], BF16)
+
+        def turned_sum(name, tag, bufs, terms):
+            acc = psum.tile([P, S], F32, name=name, tag=tag, bufs=bufs)
+            for k in range(S // P):
+                cols = slice(P * k, P * (k + 1))
+                for i, term in enumerate(terms):
+                    nc.tensor.matmul(
+                        acc[:, cols], lhsT=term[:, cols], rhs=ident[:], is_transpose=True,
+                        start=(i == 0), stop=(i == len(terms) - 1),
+                    )
+            return acc
 
         def project(t):
             dwin[t] = sb("dwin%d" % t, [P, 2 * S], F32)
             ywin[t] = sb("ywin%d" % t, [P, 2 * S], F32)
+            nc.scalar.copy(dwin[t][:, :S], product("d_ps", w2c, w2p, t, c_two, s_two)[:])
+            nc.scalar.copy(ywin[t][:, :S], product("y_ps", w1c, w1p, t, c_offs, s_offs)[:])
+
+        def project_b(t):
             bwin[t] = sb("bwin%d" % t, [P, S], F32)
-            d_ps = product("d_ps", w2c, w2p, t, c_two, s_two)
-            y_ps = product("y_ps", w1c, w1p, t, c_offs, s_offs)
-            b_ps = product("b_ps", w3c, w3p, t, c_three, s_three)
-            nc.scalar.copy(dwin[t][:, :S], d_ps[:])
-            nc.scalar.copy(ywin[t][:, S:], d_ps[:])
-            nc.scalar.copy(dwin[t][:, S:], y_ps[:])
-            nc.scalar.copy(ywin[t][:, :S], y_ps[:])
-            nc.scalar.copy(bwin[t][:], b_ps[:])
+            y_t[t] = sb("y_t%d" % t, [P, S], F32)
+            nc.scalar.copy(bwin[t][:], product("b_ps", w3c, w3p, t, c_three, s_three)[:])
+            nc.scalar.copy(y_t[t][:], turned_sum("yt_ps", "yt", 1, [ywin[t]])[:])
 
         def gate(t):
-            u[t] = sb("u%d" % t, [P, S], F32)
-            sg[t] = sb("sg%d" % t, [P, S], F32)
-            nc.vector.tensor_tensor(u[t][:], dwin[t][:].indirect(l_n2[:]), ywin[t][:, S:], ALU.subtract)
-            nc.scalar.activation(sg[t][:], u[t][:], ACT.Sigmoid)
+            dg[t] = sb("dg%d" % t, [P, S], F32)
+            s_t[t] = sb("s_t%d" % t, [P, S], F32)
+            nc.vector.tensor_scalar(dg[t][:], dwin[t][:].indirect(l_n2[:]), -1.0, 0.0, ALU.mult, ALU.add)
+            nc.scalar.activation(s_t[t][:], turned_sum("ut_ps", "ut", 1, [dwin[t], dg[t]])[:], ACT.Sigmoid, scale=-1.0)
 
         def pull(t):
-            e[t] = sb("e%d" % t, [P, S], F32)
-            nc.vector.tensor_tensor(e[t][:], ywin[t][:].indirect(l_n1[:]), dwin[t][:, S:], ALU.subtract)
+            yg[t] = sb("yg%d" % t, [P, S], F32)
+            nc.vector.tensor_scalar(yg[t][:], ywin[t][:].indirect(l_n1[:]), -1.0, 0.0, ALU.mult, ALU.add)
+            e_t[t] = turned_sum("et_ps", "et", 2, [ywin[t], yg[t]])
 
         def fetch_b(t):
             bg[t] = sb("bg%d" % t, [P, W], F32)
             nc.vector.tensor_copy(bg[t][:], bwin[t][:].indirect(l_n4[:]))
 
-        def gated(t):
-            pr[t] = sb("pr%d" % t, [P, S], F32)
-            nc.vector.tensor_tensor(pr[t][:], sg[t][:], e[t][:], ALU.mult)
-
         def mix(t):
-            m1[t] = sb("m1_%d" % t, [P, S], F32)
+            p_t[t] = sb("p_t%d" % t, [P, S], F32)
             ds[t] = sb("ds%d" % t, [P, S], F32)
-            nc.vector.tensor_tensor(m1[t][:], pr[t][:], dwin[t][:, S:], ALU.add)
-            nc.scalar.copy(ds[t][:], m1[t][:])
-
-        def fetch_m(t):
-            mg[t] = sb("mg%d" % t, [P, W], F32)
-            nc.vector.tensor_scalar(mg[t][:], m1[t][:].indirect(l_n3[:]), -0.5, 0.0, ALU.mult, ALU.add)
+            nc.vector.scalar_tensor_tensor(p_t[t][:], e_t[t][:], -1.0, s_t[t][:], ALU.mult, ALU.mult)
+            nc.scalar.copy(ds[t][:], turned_sum("m1_ps", "m1", 2, [y_t[t], p_t[t]])[:])
 
         def put(t):
+            mg[t] = sb("mg%d" % t, [P, W], F32)
+            nc.vector.tensor_scalar(mg[t][:], ds[t][:].indirect(l_n3[:]), -0.5, 0.0, ALU.mult, ALU.add)
             nc.vector.tensor_tensor(ds[t][:].indirect(l_n3[:]), bg[t][:], mg[t][:], ALU.add)
             nc.scalar.activation(z[:, :, t], ds[t][:], ACT.Copy, scale=gain[:, t : t + 1])
 
@@ -197,26 +205,21 @@ def tile_picked_triopullbputbpagex_none_po_kernel(
         project(1)
         gate(0)
         pull(0)
-        fetch_b(0)
         for t in range(PACK):
-            gated(t)
             if t + 2 < PACK:
                 project(t + 2)
+            project_b(t)
             if t < last:
                 gate(t + 1)
-            else:
-                w4c = deal_words("w4c", w4_raw)
-            mix(t)
-            if t < last:
                 pull(t + 1)
-            else:
-                w4p = deal_scales("w4p", w4s_raw)
-            fetch_m(t)
-            if t < last:
-                fetch_b(t + 1)
-            else:
-                fetch_page(0, "pr%d" % last)
-            put(t)
+            fetch_b(t)
+            mix(t)
+            if t > 0:
+                put(t - 1)
+        w4c = deal_words("w4c", w4_raw)
+        w4p = deal_scales("w4p", w4s_raw)
+        fetch_page(0, "s_t%d" % last)
+        put(last)
 
         fetch_page(1, "bg%d" % last)
         fetch_page(2, "mg%d" % last)
@@ -226,7 +229,7 @@ def tile_picked_triopullbputbpagex_none_po_kernel(
         fetch_page(3, "z")
 
         woven = [sb("woven%d" % i, [P, n, PACK], BF16) for i, (c0, n) in enumerate(CHUNKS)]
-        h_ps = [product("h_ps", w4c, w4p, t, z_codes, z_planes) for t in range(PACK)]
+        h_ps = [product("h_ps", w4c, w4p, t, z_codes, z_planes, "acc" if t < 2 else "et") for t in range(PACK)]
         nw = {}
 
         def larger(t):
@@ -256,4 +259,4 @@ def tile_picked_triopullbputbpagex_none_po_kernel(
             )
             nc.sync.dma_start(words_out[:, c0 : c0 + n], o_codes[:].bitcast(I32))
         for q in range(QUADS):
-            nc.sync.dma_start(out_2[0, 4 * q : 4 * q + 4, :].bitcast(I32), o_planes[32 * q : 32 * q + 4, :].bitcast(I32))
+            (nc.sync if q < 2 else nc.scalar).dma_start(out_2[0, 4 * q : 4 * q + 4, :].bitcast(I32), o_planes[32 * q : 32 * q + 4, :].bitcast(I32))

@@ -20,6 +20,8 @@ ACT = mybir.ActivationFunctionType
 P = 128
 PACK = 4
 QUADS = 4
+RUNS = 8
+TURN = 2
 CHUNKS = ((0, 512), (512, 256), (768, 256))
 
 
@@ -32,8 +34,8 @@ def tile_picked_triopullbputbpagex_none_po_kernel(
         keep = ctx.enter_context(tc.tile_pool(name="keep", bufs=1))
         psum = ctx.enter_context(tc.psum_pool(name="psum", bufs=1))
 
-        def sb(name, shape, dtype, tag=None):
-            return keep.tile(shape, dtype, name=name, tag=tag or name, align_bytes=64)
+        def sb(name, shape, dtype, tag=None, bufs=1):
+            return keep.tile(shape, dtype, name=name, tag=tag or name, bufs=bufs, align_bytes=64)
 
         def load_list(name, src):
             lst = keep.tile(list(src.shape), U16, name=name)
@@ -45,42 +47,48 @@ def tile_picked_triopullbputbpagex_none_po_kernel(
             engine.memset(rows[:].bitcast(I32), 0)
             return rows
 
-        def load_scale_rows(rows, src):
+        def load_scale_rows(rows, src, queue=nc.sync):
             for q in range(QUADS):
-                nc.sync.dma_start(rows[32 * q : 32 * q + 4, :].bitcast(I32), src[0, 4 * q : 4 * q + 4, :].bitcast(I32))
+                queue.dma_start(rows[32 * q : 32 * q + 4, :].bitcast(I32), src[0, 4 * q : 4 * q + 4, :].bitcast(I32))
 
-        def load_words(name, src):
-            raw = sb(name, [P, 2 * H], U8)
+        def load_words(name, src, tag=None):
+            raw = sb(name, [P, 2 * H], U8, tag=tag)
             nc.sync.dma_start(raw[:].bitcast(I32), src[0].bitcast(I32))
             return raw
 
-        def deal_words(name, raw):
-            dealt = sb(name, [P, 2 * H], U8)
-            nc.vector.tensor_copy(
-                out=dealt[:].rearrange("p (t m b) -> p t m b", t=PACK, b=2),
-                in_=raw[:].rearrange("p (m t b) -> p t m b", t=PACK, b=2),
-            )
-            return dealt
+        def deal_runs(name, words, rows):
+            codes = sb(name + "_codes", [P, 2 * H], U8)
+            planes = sb(name + "_planes", [P, H], U8)
+            for dst, src in ((codes, words), (planes, rows)):
+                nc.gpsimd.tensor_copy(
+                    out=dst[:].bitcast(I32).rearrange("p (j r w) -> p j r w", j=PACK, r=RUNS),
+                    in_=src[:].bitcast(I32).rearrange("p (r j w) -> p j r w", j=PACK, r=RUNS),
+                )
+            return codes, planes
 
-        def deal_scales(name, raw):
-            dealt = sb(name, [P, H], U8)
+        def deal_fours(name, words, rows, tags):
+            codes = sb(name + "_codes", [P, 2 * N], U8, tag=tags[0])
+            planes = sb(name + "_planes", [P, N], U8, tag=tags[1])
             nc.vector.tensor_copy(
-                out=dealt[:].rearrange("p (t m) -> p t m", t=PACK),
-                in_=raw[:].rearrange("p (m t) -> p t m", t=PACK),
+                out=planes[:].rearrange("p (t m) -> p t m", t=PACK), in_=rows[:].rearrange("p (m t) -> p t m", t=PACK)
             )
-            return dealt
+            nc.vector.tensor_copy(
+                out=codes[:].rearrange("p (t m b) -> p t m b", t=PACK, b=2),
+                in_=words[:].rearrange("p (m t b) -> p t m b", t=PACK, b=2),
+            )
+            return codes, planes
 
         def pick(name, table, lst, dtype):
             picked = sb(name, [P, S], dtype)
             nc.vector.tensor_copy(picked[:], table[:].indirect(lst[:]))
             return picked
 
-        def product(name, w_codes, w_planes, t, codes, planes, tag="acc"):
-            acc = psum.tile([P, S], F32, name=name, tag=tag, bufs=2)
+        def product(name, dealt, t, codes, planes, tag="acc", bufs=3):
+            acc = psum.tile([P, S], F32, name=name, tag=tag, bufs=bufs)
             nc.tensor.matmul_mx(
                 out=acc[:],
-                lhsT=w_codes[:, 2 * P * t : 2 * P * (t + 1)].bitcast(FP4X4),
-                lhsT_scale=w_planes[:, P * t : P * (t + 1)],
+                lhsT=dealt[0][:, 2 * P * t : 2 * P * (t + 1)].bitcast(FP4X4),
+                lhsT_scale=dealt[1][:, P * t : P * (t + 1)],
                 rhs=codes[:].bitcast(FP8X4),
                 rhs_scale=planes[:],
                 start=True,
@@ -88,111 +96,125 @@ def tile_picked_triopullbputbpagex_none_po_kernel(
             )
             return acc
 
-        xs = scale_tile("xs", T, nc.gpsimd)
-        w2s_raw = scale_tile("w2s_raw", H, nc.gpsimd)
-        w1s_raw = scale_tile("w1s_raw", H, nc.gpsimd)
-        w3s_raw = scale_tile("w3s_raw", H, nc.gpsimd)
-        w4s_raw = scale_tile("w4s_raw", N, nc.gpsimd)
+        xs = scale_tile("xs", T, nc.vector)
+        w2s_raw = scale_tile("w2s_raw", H, nc.vector)
+        w1s_raw = scale_tile("w1s_raw", H, nc.vector)
+        w3s_raw = scale_tile("w3s_raw", H, nc.vector)
+        w4s_raw = scale_tile("w4s_raw", N, nc.vector)
         warm = sb("warm", [P, 1], F32)
         warm2 = sb("warm2", [P, 1], F32)
         nc.gpsimd.memset(warm[:], 0.0)
         ident = sb("ident", [P, P], F32)
         make_identity(nc, ident[:])
-        nc.scalar.activation(warm2[:], warm[:], ACT.Sigmoid)
+        ident_bf = sb("ident_bf", [P, P], BF16)
+        make_identity(nc, ident_bf[:])
+        gain_rows = sb("gain_rows", [P, P], F32)
+        nc.gpsimd.memset(gain_rows[:], 0.0)
 
-        load_scale_rows(xs, x_scales)
         l_two = load_list("l_two", two)
-        w2_raw = load_words("w2_raw", w2_words)
         l_offs = load_list("l_offs", offs)
+        w2_raw = load_words("w2_raw", w2_words)
+        load_scale_rows(xs, x_scales)
         xw = sb("xw", [P, T], U32)
         nc.sync.dma_start(xw[:].bitcast(I32), x_words[0].rearrange("p n t -> p (n t)").bitcast(I32))
-        w1_raw = load_words("w1_raw", w1_words)
         load_scale_rows(w2s_raw, w2_scales)
-        l_three = load_list("l_three", three)
+        w1_raw = load_words("w1_raw", w1_words)
         load_scale_rows(w1s_raw, w1_scales)
-        w3_raw = load_words("w3_raw", w3_words)
+        l_three = load_list("l_three", three)
         l_n2 = load_list("l_n2", n2)
         l_n1 = load_list("l_n1", n1)
+        w3_raw = load_words("w3_raw", w3_words)
         load_scale_rows(w3s_raw, w3_scales)
         l_n4 = load_list("l_n4", n4)
         l_n3 = load_list("l_n3", n3)
-        gain = sb("gain", [P, PACK], F32)
-        nc.sync.dma_start(gain[:], gn.rearrange("(p t) o -> p (t o)", t=PACK))
+        nc.sync.dma_start(
+            gain_rows[:PACK, :].rearrange("j (r i) -> j r i", r=RUNS), gn.rearrange("(r j i) o -> j r (i o)", r=RUNS, j=PACK)
+        )
         l_n5 = load_list("l_n5", n5)
-        w4_raw = load_words("w4_raw", w4_words)
-        load_scale_rows(w4s_raw, w4_scales)
-        mem_rows = mem.rearrange("(p t) u -> p t u", t=PACK)
-        out_rows = out_0.rearrange("(p t) u -> p t u", t=PACK)
-        page = []
-        for t in range(PACK):
-            page.append(sb("page%d" % t, [P, U], F32))
-            nc.sync.dma_start(page[t][:], mem_rows[:, t, :])
 
+        nc.scalar.activation(warm2[:], warm[:], ACT.Sigmoid)
         s_two = pick("s_two", xs, l_two, U8)
-        w2c = deal_words("w2c", w2_raw)
         s_offs = pick("s_offs", xs, l_offs, U8)
         c_two = pick("c_two", xw, l_two, U32)
-        w2p = deal_scales("w2p", w2s_raw)
         c_offs = pick("c_offs", xw, l_offs, U32)
-        w1c = deal_words("w1c", w1_raw)
-        w1p = deal_scales("w1p", w1s_raw)
         s_three = pick("s_three", xs, l_three, U8)
         c_three = pick("c_three", xw, l_three, U32)
-        w3c = deal_words("w3c", w3_raw)
-        w3p = deal_scales("w3p", w3s_raw)
 
-        dwin, ywin, bwin, y_t, dg, yg, s_t, e_t, bg, p_t, ds, mg = ({} for i in range(12))
+        w2 = deal_runs("w2", w2_raw, w2s_raw)
+        w1 = deal_runs("w1", w1_raw, w1s_raw)
+        w3 = deal_runs("w3", w3_raw, w3s_raw)
+
+        d_own, y_own, dwin, ywin, bwin, sg, e, bg, ds, mg = ({} for i in range(10))
         z = sb("z", [P, S, PACK], BF16)
+        z_turned = sb("z_turned", [P, S // P, 2, P], F32)
 
-        def turned_sum(name, tag, bufs, terms):
-            acc = psum.tile([P, S], F32, name=name, tag=tag, bufs=bufs)
+        def turned_sum(name, tag, terms, dtype=F32):
+            acc = psum.tile([P, S], dtype, name=name, tag=tag)
             for k in range(S // P):
                 cols = slice(P * k, P * (k + 1))
                 for i, term in enumerate(terms):
                     nc.tensor.matmul(
-                        acc[:, cols], lhsT=term[:, cols], rhs=ident[:], is_transpose=True,
+                        acc[:, cols], lhsT=term[:, cols], rhs=(ident if dtype == F32 else ident_bf)[:], is_transpose=True,
                         start=(i == 0), stop=(i == len(terms) - 1),
                     )
             return acc
 
-        def project(t):
-            dwin[t] = sb("dwin%d" % t, [P, 2 * S], F32)
-            ywin[t] = sb("ywin%d" % t, [P, 2 * S], F32)
-            nc.scalar.copy(dwin[t][:, :S], product("d_ps", w2c, w2p, t, c_two, s_two)[:])
-            nc.scalar.copy(ywin[t][:, :S], product("y_ps", w1c, w1p, t, c_offs, s_offs)[:])
+        def project(name, t, dealt, codes, planes):
+            win = sb("%swin%d" % (name, t), [P, 2 * S], F32)
+            own = sb("%s_own%d" % (name, t), [P, S], F32)
+            acc = product(name + "_ps", dealt, t, codes, planes)
+            nc.scalar.copy(win[:, :S], acc[:])
+            if t == 0:
+                nc.scalar.copy(own[:], acc[:])
+            else:
+                nc.sync.dma_start(own[:], win[:, :S])
+            return win, own
+
+        def project_d(t):
+            dwin[t], d_own[t] = project("d", t, w2, c_two, s_two)
+
+        def project_y(t):
+            ywin[t], y_own[t] = project("y", t, w1, c_offs, s_offs)
 
         def project_b(t):
             bwin[t] = sb("bwin%d" % t, [P, S], F32)
-            y_t[t] = sb("y_t%d" % t, [P, S], F32)
-            nc.scalar.copy(bwin[t][:], product("b_ps", w3c, w3p, t, c_three, s_three)[:])
-            nc.scalar.copy(y_t[t][:], turned_sum("yt_ps", "yt", 1, [ywin[t]])[:])
+            nc.scalar.copy(bwin[t][:], product("b_ps", w3, t, c_three, s_three)[:])
 
         def gate(t):
-            dg[t] = sb("dg%d" % t, [P, S], F32)
-            s_t[t] = sb("s_t%d" % t, [P, S], F32)
-            nc.vector.tensor_scalar(dg[t][:], dwin[t][:].indirect(l_n2[:]), -1.0, 0.0, ALU.mult, ALU.add)
-            nc.scalar.activation(s_t[t][:], turned_sum("ut_ps", "ut", 1, [dwin[t], dg[t]])[:], ACT.Sigmoid, scale=-1.0)
+            u = sb("u%d" % t, [P, S], F32)
+            sg[t] = sb("sg%d" % t, [P, S], F32, tag="turn", bufs=TURN)
+            nc.vector.tensor_tensor(u[:], dwin[t][:].indirect(l_n2[:]), d_own[t][:], ALU.subtract)
+            nc.scalar.activation(sg[t][:], u[:], ACT.Sigmoid)
 
         def pull(t):
-            yg[t] = sb("yg%d" % t, [P, S], F32)
-            nc.vector.tensor_scalar(yg[t][:], ywin[t][:].indirect(l_n1[:]), -1.0, 0.0, ALU.mult, ALU.add)
-            e_t[t] = turned_sum("et_ps", "et", 2, [ywin[t], yg[t]])
+            e[t] = sb("e%d" % t, [P, S], F32)
+            nc.vector.tensor_tensor(e[t][:], ywin[t][:].indirect(l_n1[:]), y_own[t][:], ALU.subtract)
 
         def fetch_b(t):
             bg[t] = sb("bg%d" % t, [P, W], F32)
             nc.vector.tensor_copy(bg[t][:], bwin[t][:].indirect(l_n4[:]))
 
         def mix(t):
-            p_t[t] = sb("p_t%d" % t, [P, S], F32)
+            pr = sb("pr%d" % t, [P, S], F32)
+            m1_turned = sb("m1_turned%d" % t, [P, S], F32, tag="mid")
             ds[t] = sb("ds%d" % t, [P, S], F32)
-            nc.vector.scalar_tensor_tensor(p_t[t][:], e_t[t][:], -1.0, s_t[t][:], ALU.mult, ALU.mult)
-            nc.scalar.copy(ds[t][:], turned_sum("m1_ps", "m1", 2, [y_t[t], p_t[t]])[:])
+            nc.vector.tensor_tensor(pr[:], sg[t][:], e[t][:], ALU.mult)
+            nc.scalar.copy(m1_turned[:], turned_sum("m1t_ps", "m1t", [ywin[t], pr])[:])
+            nc.scalar.copy(ds[t][:], turned_sum("m1_ps", "m1", [m1_turned])[:])
+
+        def fetch_m(t):
+            mg[t] = sb("mg%d" % t, [P, W], F32, tag="turn", bufs=TURN)
+            nc.vector.tensor_scalar(mg[t][:], ds[t][:].indirect(l_n3[:]), -0.5, 0.0, ALU.mult, ALU.add)
 
         def put(t):
-            mg[t] = sb("mg%d" % t, [P, W], F32)
-            nc.vector.tensor_scalar(mg[t][:], ds[t][:].indirect(l_n3[:]), -0.5, 0.0, ALU.mult, ALU.add)
             nc.vector.tensor_tensor(ds[t][:].indirect(l_n3[:]), bg[t][:], mg[t][:], ALU.add)
-            nc.scalar.activation(z[:, :, t], ds[t][:], ACT.Copy, scale=gain[:, t : t + 1])
+            z_rows = sb("z_rows%d" % t, [P, S], BF16, tag="mid")
+            nc.scalar.activation(z_rows[:], ds[t][:], ACT.Copy, scale=gain[:, t : t + 1])
+            zt_ps = turned_sum("zt_ps", "zt", [z_rows], BF16)
+            nc.scalar.copy(
+                z_turned[:].rearrange("c k u (r j a) -> c j k u r a", r=RUNS, j=PACK)[:, t],
+                zt_ps[:].bitcast(F32).rearrange("c (k r a u) -> c k u r a", r=RUNS, a=4, u=2),
+            )
 
         half = {}
 
@@ -201,35 +223,60 @@ def tile_picked_triopullbputbpagex_none_po_kernel(
             nc.vector.tensor_scalar(half[t][:], page[t][:].indirect(l_n5[:]), 0.5, 0.0, ALU.mult, ALU.add)
 
         last = PACK - 1
-        project(0)
-        project(1)
+        gain_ps = psum.tile([P, P], F32, name="gain_ps", tag="m1")
+        nc.tensor.transpose(gain_ps[:], gain_rows[:], ident[:])
+        gain = sb("gain", [P, PACK], F32)
+        nc.scalar.copy(gain[:], gain_ps[:, :PACK])
+        project_d(0)
+        project_d(1)
+        project_y(0)
+        project_y(1)
         gate(0)
         pull(0)
         for t in range(PACK):
             if t + 2 < PACK:
-                project(t + 2)
+                project_d(t + 2)
+                project_y(t + 2)
             project_b(t)
             if t < last:
                 gate(t + 1)
                 pull(t + 1)
             fetch_b(t)
             mix(t)
-            if t > 0:
-                put(t - 1)
-        w4c = deal_words("w4c", w4_raw)
-        w4p = deal_scales("w4p", w4s_raw)
-        fetch_page(0, "s_t%d" % last)
-        put(last)
+        w4_raw = load_words("w4_raw", w4_words, "xs")
+        load_scale_rows(w4s_raw, w4_scales)
+        mem_rows = mem.rearrange("(p t) u -> p t u", t=PACK)
+        out_rows = out_0.rearrange("(p t) u -> p t u", t=PACK)
+        page = []
+        for t in range(PACK):
+            page.append(sb("page%d" % t, [P, U], F32, tag="ywin%d" % t))
+            nc.sync.dma_start(page[t][:], mem_rows[:, t, :])
 
-        fetch_page(1, "bg%d" % last)
-        fetch_page(2, "mg%d" % last)
+        fetch_m(0)
+        for t in range(PACK):
+            if t < last:
+                fetch_m(t + 1)
+            put(t)
+
+        for t in range(last):
+            fetch_page(t, "ds%d" % t)
+        w4 = deal_fours("w4", w4_raw, w4s_raw, ("bg%d" % last, "ds%d" % last))
+        for g in range(2):
+            back_ps = psum.tile([P, 2, 2, P], F32, name="back_ps", tag="back", bufs=2)
+            for k in range(2):
+                for u in range(2):
+                    nc.tensor.transpose(back_ps[:, k, u, :], z_turned[:, 2 * g + k, u, :], ident[:])
+            nc.scalar.copy(
+                z[:, 2 * P * g : 2 * P * (g + 1), :].bitcast(F32).rearrange("p (k c) u -> p k c u", k=2),
+                back_ps[:].rearrange("p k u c -> p k c u"),
+            )
         z_codes = sb("z_codes", [P, S], U32)
         z_planes = sb("z_planes", [P, S], U8)
         nc.vector.quantize_mx(out=z_codes[:].bitcast(FP8X4), scales=z_planes[:], in_=z[:].rearrange("p c t -> p (c t)"))
         fetch_page(3, "z")
 
         woven = [sb("woven%d" % i, [P, n, PACK], BF16) for i, (c0, n) in enumerate(CHUNKS)]
-        h_ps = [product("h_ps", w4c, w4p, t, z_codes, z_planes, "acc" if t < 2 else "et") for t in range(PACK)]
+        h_ps = [product("h_ps", w4, t, z_codes, z_planes, *(("acc", 3) if t < last else ("m1t", 1))) for t in range(PACK)]
         nw = {}
 
         def larger(t):

@@ -23,6 +23,7 @@ QUADS = 4
 RUNS = 8
 TURN = 2
 CHUNKS = ((0, 512), (512, 256), (768, 256))
+SPLIT = 512
 
 
 def tile_picked_triopullbputbpagex_none_po_kernel(
@@ -83,8 +84,8 @@ def tile_picked_triopullbputbpagex_none_po_kernel(
             nc.vector.tensor_copy(picked[:], table[:].indirect(lst[:]))
             return picked
 
-        def product(name, dealt, t, codes, planes, tag="acc", bufs=3):
-            acc = psum.tile([P, S], F32, name=name, tag=tag, bufs=bufs)
+        def product(name, dealt, t, codes, planes):
+            acc = psum.tile([P, S], F32, name=name, tag="acc", bufs=4)
             nc.tensor.matmul_mx(
                 out=acc[:],
                 lhsT=dealt[0][:, 2 * P * t : 2 * P * (t + 1)].bitcast(FP4X4),
@@ -144,12 +145,12 @@ def tile_picked_triopullbputbpagex_none_po_kernel(
         w1 = deal_runs("w1", w1_raw, w1s_raw)
         w3 = deal_runs("w3", w3_raw, w3s_raw)
 
-        d_own, y_own, dwin, ywin, bwin, sg, e, bg, ds, mg = ({} for i in range(10))
+        dd, d_own, y_own, dwin, ywin, bwin, sg, e, bg, ds, mg = ({} for i in range(11))
         z = sb("z", [P, S, PACK], BF16)
         z_turned = sb("z_turned", [P, S // P, 2, P], F32)
 
         def turned_sum(name, tag, terms, dtype=F32):
-            acc = psum.tile([P, S], dtype, name=name, tag=tag)
+            acc = psum.tile([P, S], dtype, name=name, tag=tag, bufs={"m1t": 2, "m1": 2}[tag])
             for k in range(S // P):
                 cols = slice(P * k, P * (k + 1))
                 for i, term in enumerate(terms):
@@ -164,7 +165,7 @@ def tile_picked_triopullbputbpagex_none_po_kernel(
             own = sb("%s_own%d" % (name, t), [P, S], F32)
             acc = product(name + "_ps", dealt, t, codes, planes)
             nc.scalar.copy(win[:, :S], acc[:])
-            if t == 0:
+            if name + str(t) in ("d0","y0",):
                 nc.scalar.copy(own[:], acc[:])
             else:
                 nc.sync.dma_start(own[:], win[:, :S])
@@ -180,37 +181,35 @@ def tile_picked_triopullbputbpagex_none_po_kernel(
             bwin[t] = sb("bwin%d" % t, [P, S], F32)
             nc.scalar.copy(bwin[t][:], product("b_ps", w3, t, c_three, s_three)[:])
 
+        def gate_in(t):
+            dd[t] = sb("u%d" % t, [P, S], F32)
+            nc.vector.tensor_tensor(dd[t][:], dwin[t][:].indirect(l_n2[:]), d_own[t][:], ALU.subtract)
+
         def gate(t):
-            u = sb("u%d" % t, [P, S], F32)
-            sg[t] = sb("sg%d" % t, [P, S], F32, tag="turn", bufs=TURN)
-            nc.vector.tensor_tensor(u[:], dwin[t][:].indirect(l_n2[:]), d_own[t][:], ALU.subtract)
-            nc.scalar.activation(sg[t][:], u[:], ACT.Sigmoid)
+            nc.scalar.activation(gates[:, t, :], dd[t][:], ACT.Sigmoid)
 
         def pull(t):
             e[t] = sb("e%d" % t, [P, S], F32)
             nc.vector.tensor_tensor(e[t][:], ywin[t][:].indirect(l_n1[:]), y_own[t][:], ALU.subtract)
 
         def fetch_b(t):
-            bg[t] = sb("bg%d" % t, [P, W], F32)
-            nc.vector.tensor_copy(bg[t][:], bwin[t][:].indirect(l_n4[:]))
+            nc.vector.tensor_copy(b_picked[:, t, :], bwin[t][:].indirect(l_n4[:]))
 
         def mix(t):
-            pr = sb("pr%d" % t, [P, S], F32)
-            m1_turned = sb("m1_turned%d" % t, [P, S], F32, tag="mid")
+            pr = gated[:, t, :]
+            m1_turned = sb("m1_turned%d" % t, [P, S], F32)
             ds[t] = sb("ds%d" % t, [P, S], F32)
-            nc.vector.tensor_tensor(pr[:], sg[t][:], e[t][:], ALU.mult)
-            nc.scalar.copy(m1_turned[:], turned_sum("m1t_ps", "m1t", [ywin[t], pr])[:])
+            nc.vector.tensor_tensor(pr, gates[:, t, :], e[t][:], ALU.mult)
+            nc.scalar.copy(m1_turned[:], turned_sum("m1t_ps", "m1t", [pr, ywin[t]])[:])
             nc.scalar.copy(ds[t][:], turned_sum("m1_ps", "m1", [m1_turned])[:])
 
         def fetch_m(t):
-            mg[t] = sb("mg%d" % t, [P, W], F32, tag="turn", bufs=TURN)
-            nc.vector.tensor_scalar(mg[t][:], ds[t][:].indirect(l_n3[:]), -0.5, 0.0, ALU.mult, ALU.add)
+            nc.vector.tensor_scalar(m_picked[:, t, :], ds[t][:].indirect(l_n3[:]), -0.5, 0.0, ALU.mult, ALU.add)
 
         def put(t):
-            nc.vector.tensor_tensor(ds[t][:].indirect(l_n3[:]), bg[t][:], mg[t][:], ALU.add)
-            z_rows = sb("z_rows%d" % t, [P, S], BF16, tag="mid")
-            nc.scalar.activation(z_rows[:], ds[t][:], ACT.Copy, scale=gain[:, t : t + 1])
-            zt_ps = turned_sum("zt_ps", "zt", [z_rows], BF16)
+            nc.vector.tensor_tensor(ds[t][:].indirect(l_n3[:]), b_picked[:, t, :], m_picked[:, t, :], ALU.add)
+            nc.scalar.activation(z_rows[:, t, :], ds[t][:], ACT.Copy, scale=gain[:, t : t + 1])
+            zt_ps = turned_sum("zt_ps", "m1t", [z_rows[:, t, :]], BF16)
             nc.scalar.copy(
                 z_turned[:].rearrange("c k u (r j a) -> c j k u r a", r=RUNS, j=PACK)[:, t],
                 zt_ps[:].bitcast(F32).rearrange("c (k r a u) -> c k u r a", r=RUNS, a=4, u=2),
@@ -223,33 +222,40 @@ def tile_picked_triopullbputbpagex_none_po_kernel(
             nc.vector.tensor_scalar(half[t][:], page[t][:].indirect(l_n5[:]), 0.5, 0.0, ALU.mult, ALU.add)
 
         last = PACK - 1
-        gain_ps = psum.tile([P, P], F32, name="gain_ps", tag="m1")
+        gain_ps = psum.tile([P, P], F32, name="gain_ps", tag="m1", bufs=2)
         nc.tensor.transpose(gain_ps[:], gain_rows[:], ident[:])
         gain = sb("gain", [P, PACK], F32)
         nc.scalar.copy(gain[:], gain_ps[:, :PACK])
         project_d(0)
         project_d(1)
         project_y(0)
+        project_d(2)
         project_y(1)
-        gate(0)
-        pull(0)
+        project_d(3)
+        project_y(2)
+        project_y(3)
         for t in range(PACK):
-            if t + 2 < PACK:
-                project_d(t + 2)
-                project_y(t + 2)
+            gate_in(t)
+            pull(t)
+        gated = sb("gated", [P, PACK, S], F32, tag="d_own3")
+        gates = sb("gates", [P, PACK, S], F32, tag="w1_codes")
+        for t in range(PACK):
+            gate(t)
+        for t in range(PACK):
             project_b(t)
-            if t < last:
-                gate(t + 1)
-                pull(t + 1)
-            fetch_b(t)
             mix(t)
+        b_picked = sb("b_picked", [P, PACK, W], F32, tag="e3")
+        m_picked = sb("m_picked", [P, PACK, W], F32, tag="w1_codes")
+        z_rows = sb("z_rows", [P, PACK, S], BF16, tag="m1_turned3")
+        for t in range(PACK):
+            fetch_b(t)
         w4_raw = load_words("w4_raw", w4_words, "xs")
         load_scale_rows(w4s_raw, w4_scales)
         mem_rows = mem.rearrange("(p t) u -> p t u", t=PACK)
         out_rows = out_0.rearrange("(p t) u -> p t u", t=PACK)
         page = []
         for t in range(PACK):
-            page.append(sb("page%d" % t, [P, U], F32, tag="ywin%d" % t))
+            page.append(sb("page%d" % t, [P, U], F32, tag=("e0", "e1", "e2", "m1_turned0")[t]))
             nc.sync.dma_start(page[t][:], mem_rows[:, t, :])
 
         fetch_m(0)
@@ -260,9 +266,9 @@ def tile_picked_triopullbputbpagex_none_po_kernel(
 
         for t in range(last):
             fetch_page(t, "ds%d" % t)
-        w4 = deal_fours("w4", w4_raw, w4s_raw, ("bg%d" % last, "ds%d" % last))
+        w4 = deal_fours("w4", w4_raw, w4s_raw, ("e3", "ds%d" % last))
         for g in range(2):
-            back_ps = psum.tile([P, 2, 2, P], F32, name="back_ps", tag="back", bufs=2)
+            back_ps = psum.tile([P, 2, 2, P], F32, name="back_ps", tag="acc", bufs=4)
             for k in range(2):
                 for u in range(2):
                     nc.tensor.transpose(back_ps[:, k, u, :], z_turned[:, 2 * g + k, u, :], ident[:])
@@ -275,8 +281,8 @@ def tile_picked_triopullbputbpagex_none_po_kernel(
         nc.vector.quantize_mx(out=z_codes[:].bitcast(FP8X4), scales=z_planes[:], in_=z[:].rearrange("p c t -> p (c t)"))
         fetch_page(3, "z")
 
-        woven = [sb("woven%d" % i, [P, n, PACK], BF16) for i, (c0, n) in enumerate(CHUNKS)]
-        h_ps = [product("h_ps", w4, t, z_codes, z_planes, *(("acc", 3) if t < last else ("m1t", 1))) for t in range(PACK)]
+        woven = sb("woven", [P, U, PACK], BF16)
+        h_ps = [product("h_ps", w4, t, z_codes, z_planes) for t in range(PACK)]
         nw = {}
 
         def larger(t):
@@ -289,20 +295,23 @@ def tile_picked_triopullbputbpagex_none_po_kernel(
                 larger(t + 1)
             nc.vector.tensor_copy(page[t][:].indirect(l_n5[:]), nw[t][:])
             nc.sync.dma_start(out_rows[:, t, :], page[t][:])
-            for i, (c0, n) in enumerate(CHUNKS):
-                if t == last and i == 0:
-                    nc.vector.tensor_copy(woven[i][:, :, t], page[t][:, c0 : c0 + n])
-                elif t == last - 1 and i == 0:
-                    nc.scalar.copy(woven[i][:, :, t:], page[t][:, c0 : c0 + n].unsqueeze(2).to_broadcast([P, n, 2]))
-                else:
-                    nc.scalar.copy(woven[i][:, :, t], page[t][:, c0 : c0 + n])
+            if t < last - 1:
+                nc.scalar.copy(woven[:, :, t], page[t][:])
+            elif t < last:
+                nc.scalar.copy(woven[:, :SPLIT, t:], page[t][:, :SPLIT].unsqueeze(2).to_broadcast([P, SPLIT, 2]))
+                nc.scalar.copy(woven[:, SPLIT:, t], page[t][:, SPLIT:])
+            else:
+                nc.vector.tensor_copy(woven[:, :SPLIT, t], page[t][:, :SPLIT])
+                for c0, n in CHUNKS:
+                    if c0 >= SPLIT:
+                        nc.scalar.copy(woven[:, c0 : c0 + n, t], page[t][:, c0 : c0 + n])
 
         o_planes = sb("o_planes", [P, U], U8)
         words_out = out_1[0].rearrange("p n t -> p (n t)").bitcast(I32)
         for i, (c0, n) in enumerate(CHUNKS):
             o_codes = sb("o_codes%d" % i, [P, n], U32)
             nc.vector.quantize_mx(
-                out=o_codes[:].bitcast(FP8X4), scales=o_planes[:, c0 : c0 + n], in_=woven[i][:].rearrange("p c t -> p (c t)")
+                out=o_codes[:].bitcast(FP8X4), scales=o_planes[:, c0 : c0 + n], in_=woven[:, c0 : c0 + n, :].rearrange("p c t -> p (c t)")
             )
             nc.sync.dma_start(words_out[:, c0 : c0 + n], o_codes[:].bitcast(I32))
         for q in range(QUADS):

@@ -3,7 +3,7 @@ from contextlib import ExitStack
 import concourse.mybir as mybir
 from concourse.masks import make_identity
 
-K, T, S, N, H, W, U = 512, 2048, 512, 512, 512, 256, 1024
+T, S, N, H, W, U = 2048, 512, 512, 512, 256, 1024
 FLOPS = 4 * 2 * 512 * 512 * 512
 
 F32 = mybir.dt.float32
@@ -18,12 +18,14 @@ ALU = mybir.AluOpType
 ACT = mybir.ActivationFunctionType
 
 P = 128
-PACK = 4
+SLICES = 4
+LAST = SLICES - 1
 QUADS = 4
 RUNS = 8
-TURN = 2
-CHUNKS = ((0, 512), (512, 256), (768, 256))
-SPLIT = 512
+ON_VECTOR = 2
+PRODUCT_BANKS, SUM_BANKS = 4, 2
+VECTOR_END, GPSIMD_START = 512, 768
+CHUNKS = ((0, VECTOR_END), (VECTOR_END, GPSIMD_START - VECTOR_END), (GPSIMD_START, U - GPSIMD_START))
 
 
 def tile_picked_triopullbputbpagex_none_po_kernel(
@@ -35,76 +37,85 @@ def tile_picked_triopullbputbpagex_none_po_kernel(
         keep = ctx.enter_context(tc.tile_pool(name="keep", bufs=1))
         psum = ctx.enter_context(tc.psum_pool(name="psum", bufs=1))
 
-        def sb(name, shape, dtype, tag=None, bufs=1):
-            return keep.tile(shape, dtype, name=name, tag=tag or name, bufs=bufs, align_bytes=64)
+        def sb(name, shape, dtype, after=None):
+            return keep.tile(shape, dtype, name=name, tag=after or name, bufs=1, align_bytes=64)
 
         def load_list(name, src):
             lst = keep.tile(list(src.shape), U16, name=name)
             nc.sync.dma_start(lst[:], src)
             return lst
 
-        def scale_tile(name, width, engine):
+        def zeroed_scales(name, width):
             rows = sb(name, [P, width], U8)
-            engine.memset(rows[:].bitcast(I32), 0)
+            nc.vector.memset(rows[:].bitcast(I32), 0)
             return rows
 
-        def load_scale_rows(rows, src, queue=nc.sync):
+        def load_scales(rows, src):
             for q in range(QUADS):
-                queue.dma_start(rows[32 * q : 32 * q + 4, :].bitcast(I32), src[0, 4 * q : 4 * q + 4, :].bitcast(I32))
+                nc.sync.dma_start(rows[32 * q : 32 * q + 4, :].bitcast(I32), src[0, 4 * q : 4 * q + 4, :].bitcast(I32))
 
-        def load_words(name, src, tag=None):
-            raw = sb(name, [P, 2 * H], U8, tag=tag)
-            nc.sync.dma_start(raw[:].bitcast(I32), src[0].bitcast(I32))
-            return raw
+        def load_words(name, src, after=None):
+            words = sb(name, [P, 2 * H], U8, after)
+            nc.sync.dma_start(words[:].bitcast(I32), src[0].bitcast(I32))
+            return words
 
-        def deal_runs(name, words, rows):
-            codes = sb(name + "_codes", [P, 2 * H], U8)
-            planes = sb(name + "_planes", [P, H], U8)
-            for dst, src in ((codes, words), (planes, rows)):
+        def deal_run_order(name, words, scales):
+            dealt_words = sb(name + "_words", [P, 2 * H], U8)
+            dealt_scales = sb(name + "_scales", [P, H], U8)
+            for dst, src in ((dealt_words, words), (dealt_scales, scales)):
                 nc.gpsimd.tensor_copy(
-                    out=dst[:].bitcast(I32).rearrange("p (j r w) -> p j r w", j=PACK, r=RUNS),
-                    in_=src[:].bitcast(I32).rearrange("p (r j w) -> p j r w", j=PACK, r=RUNS),
+                    out=dst[:].bitcast(I32).rearrange("p (j r w) -> p j r w", j=SLICES, r=RUNS),
+                    in_=src[:].bitcast(I32).rearrange("p (r j w) -> p j r w", j=SLICES, r=RUNS),
                 )
-            return codes, planes
+            return dealt_words, dealt_scales
 
-        def deal_fours(name, words, rows, tags):
-            codes = sb(name + "_codes", [P, 2 * N], U8, tag=tags[0])
-            planes = sb(name + "_planes", [P, N], U8, tag=tags[1])
+        def deal_word_order(name, words, scales, words_after, scales_after):
+            dealt_words = sb(name + "_words", [P, 2 * N], U8, words_after)
+            dealt_scales = sb(name + "_scales", [P, N], U8, scales_after)
             nc.vector.tensor_copy(
-                out=planes[:].rearrange("p (t m) -> p t m", t=PACK), in_=rows[:].rearrange("p (m t) -> p t m", t=PACK)
+                out=dealt_scales[:].rearrange("p (t m) -> p t m", t=SLICES),
+                in_=scales[:].rearrange("p (m t) -> p t m", t=SLICES),
             )
             nc.vector.tensor_copy(
-                out=codes[:].rearrange("p (t m b) -> p t m b", t=PACK, b=2),
-                in_=words[:].rearrange("p (m t b) -> p t m b", t=PACK, b=2),
+                out=dealt_words[:].rearrange("p (t m b) -> p t m b", t=SLICES, b=2),
+                in_=words[:].rearrange("p (m t b) -> p t m b", t=SLICES, b=2),
             )
-            return codes, planes
+            return dealt_words, dealt_scales
 
         def pick(name, table, lst, dtype):
             picked = sb(name, [P, S], dtype)
             nc.vector.tensor_copy(picked[:], table[:].indirect(lst[:]))
             return picked
 
-        def product(name, dealt, t, codes, planes):
-            acc = psum.tile([P, S], F32, name=name, tag="acc", bufs=4)
+        def product(name, weight, t, codes, scales):
+            acc = psum.tile([P, S], F32, name=name, tag="product", bufs=PRODUCT_BANKS)
             nc.tensor.matmul_mx(
                 out=acc[:],
-                lhsT=dealt[0][:, 2 * P * t : 2 * P * (t + 1)].bitcast(FP4X4),
-                lhsT_scale=dealt[1][:, P * t : P * (t + 1)],
+                lhsT=weight[0][:, 2 * P * t : 2 * P * (t + 1)].bitcast(FP4X4),
+                lhsT_scale=weight[1][:, P * t : P * (t + 1)],
                 rhs=codes[:].bitcast(FP8X4),
-                rhs_scale=planes[:],
+                rhs_scale=scales[:],
                 start=True,
                 stop=True,
             )
             return acc
 
-        xs = scale_tile("xs", T, nc.vector)
-        w2s_raw = scale_tile("w2s_raw", H, nc.vector)
-        w1s_raw = scale_tile("w1s_raw", H, nc.vector)
-        w3s_raw = scale_tile("w3s_raw", H, nc.vector)
-        w4s_raw = scale_tile("w4s_raw", N, nc.vector)
-        warm = sb("warm", [P, 1], F32)
-        warm2 = sb("warm2", [P, 1], F32)
-        nc.gpsimd.memset(warm[:], 0.0)
+        def turned_sum(name, tag, terms, dtype, identity):
+            acc = psum.tile([P, S], dtype, name=name, tag=tag, bufs=SUM_BANKS)
+            for k in range(S // P):
+                cols = slice(P * k, P * (k + 1))
+                for i, term in enumerate(terms):
+                    nc.tensor.matmul(
+                        acc[:, cols], lhsT=term[:, cols], rhs=identity[:], is_transpose=True,
+                        start=(i == 0), stop=(i == len(terms) - 1),
+                    )
+            return acc
+
+        x_scale_rows = zeroed_scales("x_scale_rows", T)
+        w2_scale_rows = zeroed_scales("w2_scale_rows", H)
+        w1_scale_rows = zeroed_scales("w1_scale_rows", H)
+        w3_scale_rows = zeroed_scales("w3_scale_rows", H)
+        w4_scale_rows = zeroed_scales("w4_scale_rows", N)
         ident = sb("ident", [P, P], F32)
         make_identity(nc, ident[:])
         ident_bf = sb("ident_bf", [P, P], BF16)
@@ -115,204 +126,193 @@ def tile_picked_triopullbputbpagex_none_po_kernel(
         l_two = load_list("l_two", two)
         l_offs = load_list("l_offs", offs)
         w2_raw = load_words("w2_raw", w2_words)
-        load_scale_rows(xs, x_scales)
-        xw = sb("xw", [P, T], U32)
-        nc.sync.dma_start(xw[:].bitcast(I32), x_words[0].rearrange("p n t -> p (n t)").bitcast(I32))
-        load_scale_rows(w2s_raw, w2_scales)
+        load_scales(x_scale_rows, x_scales)
+        x_table = sb("x_table", [P, T], U32)
+        nc.sync.dma_start(x_table[:].bitcast(I32), x_words[0].rearrange("p n t -> p (n t)").bitcast(I32))
+        load_scales(w2_scale_rows, w2_scales)
         w1_raw = load_words("w1_raw", w1_words)
-        load_scale_rows(w1s_raw, w1_scales)
+        load_scales(w1_scale_rows, w1_scales)
         l_three = load_list("l_three", three)
         l_n2 = load_list("l_n2", n2)
         l_n1 = load_list("l_n1", n1)
         w3_raw = load_words("w3_raw", w3_words)
-        load_scale_rows(w3s_raw, w3_scales)
+        load_scales(w3_scale_rows, w3_scales)
         l_n4 = load_list("l_n4", n4)
         l_n3 = load_list("l_n3", n3)
         nc.sync.dma_start(
-            gain_rows[:PACK, :].rearrange("j (r i) -> j r i", r=RUNS), gn.rearrange("(r j i) o -> j r (i o)", r=RUNS, j=PACK)
+            gain_rows[:SLICES, :].rearrange("j (r i) -> j r i", r=RUNS),
+            gn.rearrange("(r j i) o -> j r (i o)", r=RUNS, j=SLICES),
         )
         l_n5 = load_list("l_n5", n5)
 
-        nc.scalar.activation(warm2[:], warm[:], ACT.Sigmoid)
-        s_two = pick("s_two", xs, l_two, U8)
-        s_offs = pick("s_offs", xs, l_offs, U8)
-        c_two = pick("c_two", xw, l_two, U32)
-        c_offs = pick("c_offs", xw, l_offs, U32)
-        s_three = pick("s_three", xs, l_three, U8)
-        c_three = pick("c_three", xw, l_three, U32)
+        two_scales = pick("two_scales", x_scale_rows, l_two, U8)
+        offs_scales = pick("offs_scales", x_scale_rows, l_offs, U8)
+        two_codes = pick("two_codes", x_table, l_two, U32)
+        offs_codes = pick("offs_codes", x_table, l_offs, U32)
+        three_scales = pick("three_scales", x_scale_rows, l_three, U8)
+        three_codes = pick("three_codes", x_table, l_three, U32)
 
-        w2 = deal_runs("w2", w2_raw, w2s_raw)
-        w1 = deal_runs("w1", w1_raw, w1s_raw)
-        w3 = deal_runs("w3", w3_raw, w3s_raw)
+        w2 = deal_run_order("w2", w2_raw, w2_scale_rows)
+        w1 = deal_run_order("w1", w1_raw, w1_scale_rows)
+        w3 = deal_run_order("w3", w3_raw, w3_scale_rows)
 
-        dd, d_own, y_own, dwin, ywin, bwin, sg, e, bg, ds, mg = ({} for i in range(11))
-        z = sb("z", [P, S, PACK], BF16)
+        z = sb("z", [P, S, SLICES], BF16)
         z_turned = sb("z_turned", [P, S // P, 2, P], F32)
 
-        def turned_sum(name, tag, terms, dtype=F32):
-            acc = psum.tile([P, S], dtype, name=name, tag=tag, bufs={"m1t": 2, "m1": 2}[tag])
-            for k in range(S // P):
-                cols = slice(P * k, P * (k + 1))
-                for i, term in enumerate(terms):
-                    nc.tensor.matmul(
-                        acc[:, cols], lhsT=term[:, cols], rhs=(ident if dtype == F32 else ident_bf)[:], is_transpose=True,
-                        start=(i == 0), stop=(i == len(terms) - 1),
-                    )
-            return acc
+        gain_ps = psum.tile([P, P], F32, name="gain_ps", tag="back", bufs=SUM_BANKS)
+        nc.tensor.transpose(gain_ps[:], gain_rows[:], ident[:])
+        gain = sb("gain", [P, SLICES], F32)
+        nc.scalar.copy(gain[:], gain_ps[:, :SLICES])
 
-        def project(name, t, dealt, codes, planes):
-            win = sb("%swin%d" % (name, t), [P, 2 * S], F32)
+        def project(name, t, weight, codes, scales):
+            window = sb("%s_window%d" % (name, t), [P, 2 * S], F32)
             own = sb("%s_own%d" % (name, t), [P, S], F32)
-            acc = product(name + "_ps", dealt, t, codes, planes)
-            nc.scalar.copy(win[:, :S], acc[:])
-            if name + str(t) in ("d0","y0",):
+            acc = product(name + "_ps", weight, t, codes, scales)
+            nc.scalar.activation(window[:, :S], acc[:], ACT.Copy)
+            if t == 0:
                 nc.scalar.copy(own[:], acc[:])
             else:
-                nc.sync.dma_start(own[:], win[:, :S])
-            return win, own
+                nc.sync.dma_start(own[:], window[:, :S])
+            return window, own
 
-        def project_d(t):
-            dwin[t], d_own[t] = project("d", t, w2, c_two, s_two)
+        d, y = {}, {}
+        for pair in range(0, SLICES, 2):
+            for t in (pair, pair + 1):
+                d[t] = project("d", t, w2, two_codes, two_scales)
+            for t in (pair, pair + 1):
+                y[t] = project("y", t, w1, offs_codes, offs_scales)
 
-        def project_y(t):
-            ywin[t], y_own[t] = project("y", t, w1, c_offs, s_offs)
+        d_step, y_step = [], []
+        for t in range(SLICES):
+            d_step.append(sb("d_step%d" % t, [P, S], F32))
+            nc.vector.tensor_tensor(d_step[t][:], d[t][0][:].indirect(l_n2[:]), d[t][1][:], ALU.subtract)
+            y_step.append(sb("y_step%d" % t, [P, S], F32))
+            nc.vector.tensor_tensor(y_step[t][:], y[t][0][:].indirect(l_n1[:]), y[t][1][:], ALU.subtract)
 
-        def project_b(t):
-            bwin[t] = sb("bwin%d" % t, [P, S], F32)
-            nc.scalar.copy(bwin[t][:], product("b_ps", w3, t, c_three, s_three)[:])
+        gated_early = sb("gated_early", [P, ON_VECTOR, S], F32, after="y_own1")
+        late_width = (SLICES - ON_VECTOR) * S
+        late = sb("late", [P, late_width + 2 * SLICES * W], F32, after="y_own%d" % LAST)
+        gated_late = late[:, :late_width].rearrange("p (t c) -> p t c", c=S)
+        b_picked = late[:, late_width : late_width + SLICES * W].rearrange("p (t c) -> p t c", c=W)
+        m1_picked = late[:, late_width + SLICES * W :].rearrange("p (t c) -> p t c", c=W)
+        gates = sb("gates", [P, SLICES, S], F32, after="w1_words")
+        for t in range(SLICES):
+            nc.scalar.activation(gates[:, t, :], d_step[t][:], ACT.Sigmoid)
 
-        def gate_in(t):
-            dd[t] = sb("u%d" % t, [P, S], F32)
-            nc.vector.tensor_tensor(dd[t][:], dwin[t][:].indirect(l_n2[:]), d_own[t][:], ALU.subtract)
-
-        def gate(t):
-            nc.scalar.activation(gates[:, t, :], dd[t][:], ACT.Sigmoid)
-
-        def pull(t):
-            e[t] = sb("e%d" % t, [P, S], F32)
-            nc.vector.tensor_tensor(e[t][:], ywin[t][:].indirect(l_n1[:]), y_own[t][:], ALU.subtract)
-
-        def fetch_b(t):
-            nc.vector.tensor_copy(b_picked[:, t, :], bwin[t][:].indirect(l_n4[:]))
-
-        def mix(t):
-            pr = gated[:, t, :]
+        b_window, ds = [], []
+        for t in range(SLICES):
+            b_window.append(sb("b_window%d" % t, [P, S], F32))
+            nc.scalar.copy(b_window[t][:], product("b_ps", w3, t, three_codes, three_scales)[:])
             m1_turned = sb("m1_turned%d" % t, [P, S], F32)
-            ds[t] = sb("ds%d" % t, [P, S], F32)
-            nc.vector.tensor_tensor(pr, gates[:, t, :], e[t][:], ALU.mult)
-            nc.scalar.copy(m1_turned[:], turned_sum("m1t_ps", "m1t", [pr, ywin[t]])[:])
-            nc.scalar.copy(ds[t][:], turned_sum("m1_ps", "m1", [m1_turned])[:])
+            ds.append(sb("ds%d" % t, [P, S], F32))
+            if t < ON_VECTOR:
+                gated = gated_early[:, t, :]
+                nc.vector.tensor_tensor(gated, gates[:, t, :], y_step[t][:], ALU.mult)
+            else:
+                gated = gated_late[:, t - ON_VECTOR, :]
+                nc.gpsimd.tensor_tensor(gated, gates[:, t, :], y_step[t][:], ALU.mult)
+            nc.scalar.copy(m1_turned[:], turned_sum("m1_turned_ps", "turned", [gated, y[t][0]], F32, ident)[:])
+            nc.scalar.copy(ds[t][:], turned_sum("m1_ps", "back", [m1_turned], F32, ident)[:])
 
-        def fetch_m(t):
-            nc.vector.tensor_scalar(m_picked[:, t, :], ds[t][:].indirect(l_n3[:]), -0.5, 0.0, ALU.mult, ALU.add)
+        z_rows = sb("z_rows", [P, SLICES, S], BF16, after="m1_turned%d" % LAST)
+        for t in range(SLICES):
+            nc.vector.tensor_copy(b_picked[:, t, :], b_window[t][:].indirect(l_n4[:]))
 
-        def put(t):
-            nc.vector.tensor_tensor(ds[t][:].indirect(l_n3[:]), b_picked[:, t, :], m_picked[:, t, :], ALU.add)
-            nc.scalar.activation(z_rows[:, t, :], ds[t][:], ACT.Copy, scale=gain[:, t : t + 1])
-            zt_ps = turned_sum("zt_ps", "m1t", [z_rows[:, t, :]], BF16)
-            nc.scalar.copy(
-                z_turned[:].rearrange("c k u (r j a) -> c j k u r a", r=RUNS, j=PACK)[:, t],
-                zt_ps[:].bitcast(F32).rearrange("c (k r a u) -> c k u r a", r=RUNS, a=4, u=2),
-            )
-
-        half = {}
-
-        def fetch_page(t, tag):
-            half[t] = sb("half%d" % t, [P, S], F32, tag=tag)
-            nc.vector.tensor_scalar(half[t][:], page[t][:].indirect(l_n5[:]), 0.5, 0.0, ALU.mult, ALU.add)
-
-        last = PACK - 1
-        gain_ps = psum.tile([P, P], F32, name="gain_ps", tag="m1", bufs=2)
-        nc.tensor.transpose(gain_ps[:], gain_rows[:], ident[:])
-        gain = sb("gain", [P, PACK], F32)
-        nc.scalar.copy(gain[:], gain_ps[:, :PACK])
-        project_d(0)
-        project_d(1)
-        project_y(0)
-        project_d(2)
-        project_y(1)
-        project_d(3)
-        project_y(2)
-        project_y(3)
-        for t in range(PACK):
-            gate_in(t)
-            pull(t)
-        gated = sb("gated", [P, PACK, S], F32, tag="d_own3")
-        gates = sb("gates", [P, PACK, S], F32, tag="w1_codes")
-        for t in range(PACK):
-            gate(t)
-        for t in range(PACK):
-            project_b(t)
-            mix(t)
-        b_picked = sb("b_picked", [P, PACK, W], F32, tag="e3")
-        m_picked = sb("m_picked", [P, PACK, W], F32, tag="w1_codes")
-        z_rows = sb("z_rows", [P, PACK, S], BF16, tag="m1_turned3")
-        for t in range(PACK):
-            fetch_b(t)
-        w4_raw = load_words("w4_raw", w4_words, "xs")
-        load_scale_rows(w4s_raw, w4_scales)
-        mem_rows = mem.rearrange("(p t) u -> p t u", t=PACK)
-        out_rows = out_0.rearrange("(p t) u -> p t u", t=PACK)
+        w4_raw = load_words("w4_raw", w4_words, after="x_scale_rows")
+        load_scales(w4_scale_rows, w4_scales)
+        mem_rows = mem.rearrange("(p t) u -> p t u", t=SLICES)
+        out_rows = out_0.rearrange("(p t) u -> p t u", t=SLICES)
         page = []
-        for t in range(PACK):
-            page.append(sb("page%d" % t, [P, U], F32, tag=("e0", "e1", "e2", "m1_turned0")[t]))
+        for t, done in enumerate(("d_step2", "d_step3", "y_step0", "y_step1")):
+            page.append(sb("page%d" % t, [P, U], F32, after=done))
             nc.sync.dma_start(page[t][:], mem_rows[:, t, :])
 
-        fetch_m(0)
-        for t in range(PACK):
-            if t < last:
-                fetch_m(t + 1)
-            put(t)
+        def pick_m1(t):
+            nc.vector.tensor_scalar(m1_picked[:, t, :], ds[t][:].indirect(l_n3[:]), -0.5, 0.0, ALU.mult, ALU.add)
 
-        for t in range(last):
-            fetch_page(t, "ds%d" % t)
-        w4 = deal_fours("w4", w4_raw, w4s_raw, ("e3", "ds%d" % last))
+        pick_m1(0)
+        for j in range(SLICES):
+            if j < LAST:
+                pick_m1(j + 1)
+            nc.vector.tensor_tensor(ds[j][:].indirect(l_n3[:]), b_picked[:, j, :], m1_picked[:, j, :], ALU.add)
+            nc.scalar.activation(z_rows[:, j, :], ds[j][:], ACT.Copy, scale=gain[:, j : j + 1])
+            z_ps = turned_sum("z_ps", "turned", [z_rows[:, j, :]], BF16, ident_bf)
+            nc.scalar.copy(
+                z_turned[:].rearrange("c k u (r j a) -> c j k u r a", r=RUNS, j=SLICES)[:, j],
+                z_ps[:].bitcast(F32).rearrange("c (k r a u) -> c k u r a", r=RUNS, a=4, u=2),
+            )
+
+        def pick_page(t, into):
+            nc.vector.tensor_scalar(into, page[t][:].indirect(l_n5[:]), 0.5, 0.0, ALU.mult, ALU.add)
+            return into
+
+        halves = sb("halves", [P, LAST, S], F32, after="ds0")
+        half = [pick_page(t, halves[:, t, :]) for t in range(LAST)]
+        w4 = deal_word_order("w4", w4_raw, w4_scale_rows, "y_own%d" % LAST, "ds%d" % LAST)
+
         for g in range(2):
-            back_ps = psum.tile([P, 2, 2, P], F32, name="back_ps", tag="acc", bufs=4)
+            pairs_ps = psum.tile([P, 2, 2, P], F32, name="pairs_ps", tag="product", bufs=PRODUCT_BANKS)
             for k in range(2):
                 for u in range(2):
-                    nc.tensor.transpose(back_ps[:, k, u, :], z_turned[:, 2 * g + k, u, :], ident[:])
+                    nc.tensor.transpose(pairs_ps[:, k, u, :], z_turned[:, 2 * g + k, u, :], ident[:])
             nc.scalar.copy(
                 z[:, 2 * P * g : 2 * P * (g + 1), :].bitcast(F32).rearrange("p (k c) u -> p k c u", k=2),
-                back_ps[:].rearrange("p k u c -> p k c u"),
+                pairs_ps[:].rearrange("p k u c -> p k c u"),
             )
         z_codes = sb("z_codes", [P, S], U32)
-        z_planes = sb("z_planes", [P, S], U8)
-        nc.vector.quantize_mx(out=z_codes[:].bitcast(FP8X4), scales=z_planes[:], in_=z[:].rearrange("p c t -> p (c t)"))
-        fetch_page(3, "z")
+        z_scales = sb("z_scales", [P, S], U8)
+        nc.vector.quantize_mx(out=z_codes[:].bitcast(FP8X4), scales=z_scales[:], in_=z[:].rearrange("p c t -> p (c t)"))
+        half.append(pick_page(LAST, sb("half_last", [P, S], F32, after="z")[:]))
 
-        woven = sb("woven", [P, U, PACK], BF16)
-        h_ps = [product("h_ps", w4, t, z_codes, z_planes) for t in range(PACK)]
-        nw = {}
+        h_ps = [product("h_ps", w4, t, z_codes, z_scales) for t in range(SLICES)]
+        h_rows, excess = {}, {}
+        for t in range(ON_VECTOR, SLICES):
+            h_rows[t] = sb("h_rows%d" % t, [P, S], F32)
+            over = sb("over%d" % t, [P, S], F32)
+            excess[t] = sb("excess%d" % t, [P, S], F32)
+            nc.scalar.copy(h_rows[t][:], h_ps[t][:])
+            nc.gpsimd.tensor_tensor(over[:], half[t], h_rows[t][:], ALU.subtract)
+            nc.scalar.activation(excess[t][:], over[:], ACT.Relu)
+        nw = []
+        for t in range(SLICES):
+            nw.append(sb("nw%d" % t, [P, S], F32))
+            if t < ON_VECTOR:
+                nc.vector.tensor_tensor(nw[t][:], h_ps[t][:], half[t], ALU.max)
+            else:
+                nc.gpsimd.tensor_tensor(nw[t][:], excess[t][:], h_rows[t][:], ALU.add)
 
-        def larger(t):
-            nw[t] = sb("nw%d" % t, [P, S], F32)
-            nc.vector.tensor_tensor(nw[t][:], h_ps[t][:], half[t][:], ALU.max)
+        woven = sb("woven", [P, U, SLICES], BF16, after="over%d" % LAST)
 
-        larger(0)
-        for t in range(PACK):
-            if t < last:
-                larger(t + 1)
+        def twice(rows, c0, c1):
+            return rows[:, c0:c1].unsqueeze(2).to_broadcast([P, c1 - c0, 2])
+
+        for t in range(SLICES):
             nc.vector.tensor_copy(page[t][:].indirect(l_n5[:]), nw[t][:])
             nc.sync.dma_start(out_rows[:, t, :], page[t][:])
-            if t < last - 1:
-                nc.scalar.copy(woven[:, :, t], page[t][:])
-            elif t < last:
-                nc.scalar.copy(woven[:, :SPLIT, t:], page[t][:, :SPLIT].unsqueeze(2).to_broadcast([P, SPLIT, 2]))
-                nc.scalar.copy(woven[:, SPLIT:, t], page[t][:, SPLIT:])
+            if t < LAST - 1:
+                nc.scalar.copy(woven[:, :GPSIMD_START, t], page[t][:, :GPSIMD_START])
+                nc.gpsimd.tensor_scalar(woven[:, GPSIMD_START:, t], page[t][:, GPSIMD_START:], 1.0, 0.0, ALU.mult, ALU.add)
+            elif t < LAST:
+                nc.scalar.copy(woven[:, :VECTOR_END, t:], twice(page[t], 0, VECTOR_END))
+                nc.scalar.copy(woven[:, VECTOR_END:GPSIMD_START, t], page[t][:, VECTOR_END:GPSIMD_START])
+                nc.gpsimd.tensor_scalar(
+                    woven[:, GPSIMD_START:, t:], twice(page[t], GPSIMD_START, U), 1.0, 0.0, ALU.mult, ALU.add
+                )
             else:
-                nc.vector.tensor_copy(woven[:, :SPLIT, t], page[t][:, :SPLIT])
-                for c0, n in CHUNKS:
-                    if c0 >= SPLIT:
-                        nc.scalar.copy(woven[:, c0 : c0 + n, t], page[t][:, c0 : c0 + n])
+                nc.vector.tensor_copy(woven[:, :VECTOR_END, t], page[t][:, :VECTOR_END])
+                for c0, n in CHUNKS[1:]:
+                    nc.scalar.copy(woven[:, c0 : c0 + n, t], page[t][:, c0 : c0 + n])
 
-        o_planes = sb("o_planes", [P, U], U8)
+        out_scales = sb("out_scales", [P, U], U8)
         words_out = out_1[0].rearrange("p n t -> p (n t)").bitcast(I32)
         for i, (c0, n) in enumerate(CHUNKS):
-            o_codes = sb("o_codes%d" % i, [P, n], U32)
+            out_codes = sb("out_codes%d" % i, [P, n], U32)
             nc.vector.quantize_mx(
-                out=o_codes[:].bitcast(FP8X4), scales=o_planes[:, c0 : c0 + n], in_=woven[:, c0 : c0 + n, :].rearrange("p c t -> p (c t)")
+                out=out_codes[:].bitcast(FP8X4),
+                scales=out_scales[:, c0 : c0 + n],
+                in_=woven[:, c0 : c0 + n, :].rearrange("p c t -> p (c t)"),
             )
-            nc.sync.dma_start(words_out[:, c0 : c0 + n], o_codes[:].bitcast(I32))
+            nc.sync.dma_start(words_out[:, c0 : c0 + n], out_codes[:].bitcast(I32))
         for q in range(QUADS):
-            (nc.sync if q < 2 else nc.scalar).dma_start(out_2[0, 4 * q : 4 * q + 4, :].bitcast(I32), o_planes[32 * q : 32 * q + 4, :].bitcast(I32))
+            queue = nc.sync if q < QUADS // 2 else nc.scalar
+            queue.dma_start(out_2[0, 4 * q : 4 * q + 4, :].bitcast(I32), out_scales[32 * q : 32 * q + 4, :].bitcast(I32))

from contextlib import ExitStack

import concourse.mybir as mybir
from concourse.masks import make_identity

T, S, N, H, W, U = 2048, 512, 512, 512, 256, 1024
FLOPS = 4 * 2 * 512 * 512 * 512

F32 = mybir.dt.float32
BF16 = mybir.dt.bfloat16
I32 = mybir.dt.int32
U32 = mybir.dt.uint32
U16 = mybir.dt.uint16
U8 = mybir.dt.uint8
FP8X4 = mybir.dt.float8_e4m3fn_x4
FP4X4 = mybir.dt.float4_e2m1fn_x4
ALU = mybir.AluOpType
ACT = mybir.ActivationFunctionType

P = 128
SLICES = 4
LAST = SLICES - 1
QUADS = 4
RUNS = 8
ON_VECTOR = 2
PRODUCT_BANKS, SUM_BANKS = 4, 2
VECTOR_END, GPSIMD_START = 512, 768
CHUNKS = ((0, VECTOR_END), (VECTOR_END, GPSIMD_START - VECTOR_END), (GPSIMD_START, U - GPSIMD_START))


def tile_picked_triopullbputbpagex_none_po_kernel(
    tc, x_words, x_scales, w1_words, w1_scales, w2_words, w2_scales, w3_words, w3_scales, gn,
    w4_words, w4_scales, mem, offs, two, three, n1, n2, n3, n4, n5, out_0, out_1, out_2,
):
    nc = tc.nc
    with ExitStack() as ctx:
        keep = ctx.enter_context(tc.tile_pool(name="keep", bufs=1))
        psum = ctx.enter_context(tc.psum_pool(name="psum", bufs=1))

        def sb(name, shape, dtype, after=None):
            return keep.tile(shape, dtype, name=name, tag=after or name, bufs=1, align_bytes=64)

        def load_list(name, src):
            lst = keep.tile(list(src.shape), U16, name=name)
            nc.sync.dma_start(lst[:], src)
            return lst

        def zeroed_scales(name, width):
            rows = sb(name, [P, width], U8)
            nc.vector.memset(rows[:].bitcast(I32), 0)
            return rows

        def load_scales(rows, src):
            for q in range(QUADS):
                nc.sync.dma_start(rows[32 * q : 32 * q + 4, :].bitcast(I32), src[0, 4 * q : 4 * q + 4, :].bitcast(I32))

        def load_words(name, src, after=None):
            words = sb(name, [P, 2 * H], U8, after)
            nc.sync.dma_start(words[:].bitcast(I32), src[0].bitcast(I32))
            return words

        def deal_run_order(name, words, scales):
            dealt_words = sb(name + "_words", [P, 2 * H], U8)
            dealt_scales = sb(name + "_scales", [P, H], U8)
            for dst, src in ((dealt_words, words), (dealt_scales, scales)):
                nc.gpsimd.tensor_copy(
                    out=dst[:].bitcast(I32).rearrange("p (j r w) -> p j r w", j=SLICES, r=RUNS),
                    in_=src[:].bitcast(I32).rearrange("p (r j w) -> p j r w", j=SLICES, r=RUNS),
                )
            return dealt_words, dealt_scales

        def deal_word_order(name, words, scales, words_after, scales_after):
            dealt_words = sb(name + "_words", [P, 2 * N], U8, words_after)
            dealt_scales = sb(name + "_scales", [P, N], U8, scales_after)
            nc.vector.tensor_copy(
                out=dealt_scales[:].rearrange("p (t m) -> p t m", t=SLICES),
                in_=scales[:].rearrange("p (m t) -> p t m", t=SLICES),
            )
            nc.vector.tensor_copy(
                out=dealt_words[:].rearrange("p (t m b) -> p t m b", t=SLICES, b=2),
                in_=words[:].rearrange("p (m t b) -> p t m b", t=SLICES, b=2),
            )
            return dealt_words, dealt_scales

        def pick(name, table, lst, dtype):
            picked = sb(name, [P, S], dtype)
            nc.vector.tensor_copy(picked[:], table[:].indirect(lst[:]))
            return picked

        def product(name, weight, t, codes, scales):
            acc = psum.tile([P, S], F32, name=name, tag="product", bufs=PRODUCT_BANKS)
            nc.tensor.matmul_mx(
                out=acc[:],
                lhsT=weight[0][:, 2 * P * t : 2 * P * (t + 1)].bitcast(FP4X4),
                lhsT_scale=weight[1][:, P * t : P * (t + 1)],
                rhs=codes[:].bitcast(FP8X4),
                rhs_scale=scales[:],
                start=True,
                stop=True,
            )
            return acc

        def turned_sum(name, tag, terms, dtype, identity):
            acc = psum.tile([P, S], dtype, name=name, tag=tag, bufs=SUM_BANKS)
            for k in range(S // P):
                cols = slice(P * k, P * (k + 1))
                for i, term in enumerate(terms):
                    nc.tensor.matmul(
                        acc[:, cols], lhsT=term[:, cols], rhs=identity[:], is_transpose=True,
                        start=(i == 0), stop=(i == len(terms) - 1),
                    )
            return acc

        x_scale_rows = zeroed_scales("x_scale_rows", T)
        w2_scale_rows = zeroed_scales("w2_scale_rows", H)
        w1_scale_rows = zeroed_scales("w1_scale_rows", H)
        w3_scale_rows = zeroed_scales("w3_scale_rows", H)
        w4_scale_rows = zeroed_scales("w4_scale_rows", N)
        ident = sb("ident", [P, P], F32)
        make_identity(nc, ident[:])
        ident_bf = sb("ident_bf", [P, P], BF16)
        make_identity(nc, ident_bf[:])
        gain_rows = sb("gain_rows", [P, P], F32)
        nc.gpsimd.memset(gain_rows[:], 0.0)

        l_two = load_list("l_two", two)
        l_offs = load_list("l_offs", offs)
        w2_raw = load_words("w2_raw", w2_words)
        load_scales(x_scale_rows, x_scales)
        x_table = sb("x_table", [P, T], U32)
        nc.sync.dma_start(x_table[:].bitcast(I32), x_words[0].rearrange("p n t -> p (n t)").bitcast(I32))
        load_scales(w2_scale_rows, w2_scales)
        w1_raw = load_words("w1_raw", w1_words)
        load_scales(w1_scale_rows, w1_scales)
        l_three = load_list("l_three", three)
        l_n2 = load_list("l_n2", n2)
        l_n1 = load_list("l_n1", n1)
        w3_raw = load_words("w3_raw", w3_words)
        load_scales(w3_scale_rows, w3_scales)
        l_n4 = load_list("l_n4", n4)
        l_n3 = load_list("l_n3", n3)
        nc.sync.dma_start(
            gain_rows[:SLICES, :].rearrange("j (r i) -> j r i", r=RUNS),
            gn.rearrange("(r j i) o -> j r (i o)", r=RUNS, j=SLICES),
        )
        l_n5 = load_list("l_n5", n5)

        two_scales = pick("two_scales", x_scale_rows, l_two, U8)
        offs_scales = pick("offs_scales", x_scale_rows, l_offs, U8)
        two_codes = pick("two_codes", x_table, l_two, U32)
        offs_codes = pick("offs_codes", x_table, l_offs, U32)
        three_scales = pick("three_scales", x_scale_rows, l_three, U8)
        three_codes = pick("three_codes", x_table, l_three, U32)

        w2 = deal_run_order("w2", w2_raw, w2_scale_rows)
        w1 = deal_run_order("w1", w1_raw, w1_scale_rows)
        w3 = deal_run_order("w3", w3_raw, w3_scale_rows)

        z = sb("z", [P, S, SLICES], BF16)
        z_turned = sb("z_turned", [P, S // P, 2, P], F32)

        gain_ps = psum.tile([P, P], F32, name="gain_ps", tag="back", bufs=SUM_BANKS)
        nc.tensor.transpose(gain_ps[:], gain_rows[:], ident[:])
        gain = sb("gain", [P, SLICES], F32)
        nc.scalar.copy(gain[:], gain_ps[:, :SLICES])

        def project(name, t, weight, codes, scales):
            window = sb("%s_window%d" % (name, t), [P, 2 * S], F32)
            own = sb("%s_own%d" % (name, t), [P, S], F32)
            acc = product(name + "_ps", weight, t, codes, scales)
            nc.scalar.activation(window[:, :S], acc[:], ACT.Copy)
            if t == 0:
                nc.scalar.copy(own[:], acc[:])
            else:
                nc.sync.dma_start(own[:], window[:, :S])
            return window, own

        d, y = {}, {}
        for pair in range(0, SLICES, 2):
            for t in (pair, pair + 1):
                d[t] = project("d", t, w2, two_codes, two_scales)
            for t in (pair, pair + 1):
                y[t] = project("y", t, w1, offs_codes, offs_scales)

        d_step, y_step = [], []
        for t in range(SLICES):
            d_step.append(sb("d_step%d" % t, [P, S], F32))
            nc.vector.tensor_tensor(d_step[t][:], d[t][0][:].indirect(l_n2[:]), d[t][1][:], ALU.subtract)
            y_step.append(sb("y_step%d" % t, [P, S], F32))
            nc.vector.tensor_tensor(y_step[t][:], y[t][0][:].indirect(l_n1[:]), y[t][1][:], ALU.subtract)

        gated_early = sb("gated_early", [P, ON_VECTOR, S], F32, after="y_own1")
        late_width = (SLICES - ON_VECTOR) * S
        late = sb("late", [P, late_width + 2 * SLICES * W], F32, after="y_own%d" % LAST)
        gated_late = late[:, :late_width].rearrange("p (t c) -> p t c", c=S)
        b_picked = late[:, late_width : late_width + SLICES * W].rearrange("p (t c) -> p t c", c=W)
        m1_picked = late[:, late_width + SLICES * W :].rearrange("p (t c) -> p t c", c=W)
        gates = sb("gates", [P, SLICES, S], F32, after="w1_words")
        for t in range(SLICES):
            nc.scalar.activation(gates[:, t, :], d_step[t][:], ACT.Sigmoid)

        b_window, ds = [], []
        for t in range(SLICES):
            b_window.append(sb("b_window%d" % t, [P, S], F32))
            nc.scalar.copy(b_window[t][:], product("b_ps", w3, t, three_codes, three_scales)[:])
            m1_turned = sb("m1_turned%d" % t, [P, S], F32)
            ds.append(sb("ds%d" % t, [P, S], F32))
            if t < ON_VECTOR:
                gated = gated_early[:, t, :]
                nc.vector.tensor_tensor(gated, gates[:, t, :], y_step[t][:], ALU.mult)
            else:
                gated = gated_late[:, t - ON_VECTOR, :]
                nc.gpsimd.tensor_tensor(gated, gates[:, t, :], y_step[t][:], ALU.mult)
            nc.scalar.copy(m1_turned[:], turned_sum("m1_turned_ps", "turned", [gated, y[t][0]], F32, ident)[:])
            nc.scalar.copy(ds[t][:], turned_sum("m1_ps", "back", [m1_turned], F32, ident)[:])

        z_rows = sb("z_rows", [P, SLICES, S], BF16, after="m1_turned%d" % LAST)
        for t in range(SLICES):
            nc.vector.tensor_copy(b_picked[:, t, :], b_window[t][:].indirect(l_n4[:]))

        w4_raw = load_words("w4_raw", w4_words, after="x_scale_rows")
        load_scales(w4_scale_rows, w4_scales)
        mem_rows = mem.rearrange("(p t) u -> p t u", t=SLICES)
        out_rows = out_0.rearrange("(p t) u -> p t u", t=SLICES)
        page = []
        for t, done in enumerate(("d_step2", "d_step3", "y_step0", "y_step1")):
            page.append(sb("page%d" % t, [P, U], F32, after=done))
            nc.sync.dma_start(page[t][:], mem_rows[:, t, :])

        def pick_m1(t):
            nc.vector.tensor_scalar(m1_picked[:, t, :], ds[t][:].indirect(l_n3[:]), -0.5, 0.0, ALU.mult, ALU.add)

        pick_m1(0)
        for j in range(SLICES):
            if j < LAST:
                pick_m1(j + 1)
            nc.vector.tensor_tensor(ds[j][:].indirect(l_n3[:]), b_picked[:, j, :], m1_picked[:, j, :], ALU.add)
            nc.scalar.activation(z_rows[:, j, :], ds[j][:], ACT.Copy, scale=gain[:, j : j + 1])
            z_ps = turned_sum("z_ps", "turned", [z_rows[:, j, :]], BF16, ident_bf)
            nc.scalar.copy(
                z_turned[:].rearrange("c k u (r j a) -> c j k u r a", r=RUNS, j=SLICES)[:, j],
                z_ps[:].bitcast(F32).rearrange("c (k r a u) -> c k u r a", r=RUNS, a=4, u=2),
            )

        def pick_page(t, into):
            nc.vector.tensor_scalar(into, page[t][:].indirect(l_n5[:]), 0.5, 0.0, ALU.mult, ALU.add)
            return into

        halves = sb("halves", [P, LAST, S], F32, after="ds0")
        half = [pick_page(t, halves[:, t, :]) for t in range(LAST)]
        w4 = deal_word_order("w4", w4_raw, w4_scale_rows, "y_own%d" % LAST, "ds%d" % LAST)

        for g in range(2):
            pairs_ps = psum.tile([P, 2, 2, P], F32, name="pairs_ps", tag="product", bufs=PRODUCT_BANKS)
            for k in range(2):
                for u in range(2):
                    nc.tensor.transpose(pairs_ps[:, k, u, :], z_turned[:, 2 * g + k, u, :], ident[:])
            nc.scalar.copy(
                z[:, 2 * P * g : 2 * P * (g + 1), :].bitcast(F32).rearrange("p (k c) u -> p k c u", k=2),
                pairs_ps[:].rearrange("p k u c -> p k c u"),
            )
        z_codes = sb("z_codes", [P, S], U32)
        z_scales = sb("z_scales", [P, S], U8)
        nc.vector.quantize_mx(out=z_codes[:].bitcast(FP8X4), scales=z_scales[:], in_=z[:].rearrange("p c t -> p (c t)"))
        half.append(pick_page(LAST, sb("half_last", [P, S], F32, after="z")[:]))

        h_ps = [product("h_ps", w4, t, z_codes, z_scales) for t in range(SLICES)]
        h_rows, excess = {}, {}
        for t in range(ON_VECTOR, SLICES):
            h_rows[t] = sb("h_rows%d" % t, [P, S], F32)
            over = sb("over%d" % t, [P, S], F32)
            excess[t] = sb("excess%d" % t, [P, S], F32)
            nc.scalar.copy(h_rows[t][:], h_ps[t][:])
            nc.gpsimd.tensor_tensor(over[:], half[t], h_rows[t][:], ALU.subtract)
            nc.scalar.activation(excess[t][:], over[:], ACT.Relu)
        nw = []
        for t in range(SLICES):
            nw.append(sb("nw%d" % t, [P, S], F32))
            if t < ON_VECTOR:
                nc.vector.tensor_tensor(nw[t][:], h_ps[t][:], half[t], ALU.max)
            else:
                nc.gpsimd.tensor_tensor(nw[t][:], excess[t][:], h_rows[t][:], ALU.add)

        woven = sb("woven", [P, U, SLICES], BF16, after="over%d" % LAST)

        def twice(rows, c0, c1):
            return rows[:, c0:c1].unsqueeze(2).to_broadcast([P, c1 - c0, 2])

        for t in range(SLICES):
            nc.vector.tensor_copy(page[t][:].indirect(l_n5[:]), nw[t][:])
            nc.sync.dma_start(out_rows[:, t, :], page[t][:])
            if t < LAST - 1:
                nc.scalar.copy(woven[:, :GPSIMD_START, t], page[t][:, :GPSIMD_START])
                nc.gpsimd.tensor_scalar(woven[:, GPSIMD_START:, t], page[t][:, GPSIMD_START:], 1.0, 0.0, ALU.mult, ALU.add)
            elif t < LAST:
                nc.scalar.copy(woven[:, :VECTOR_END, t:], twice(page[t], 0, VECTOR_END))
                nc.scalar.copy(woven[:, VECTOR_END:GPSIMD_START, t], page[t][:, VECTOR_END:GPSIMD_START])
                nc.gpsimd.tensor_scalar(
                    woven[:, GPSIMD_START:, t:], twice(page[t], GPSIMD_START, U), 1.0, 0.0, ALU.mult, ALU.add
                )
            else:
                nc.vector.tensor_copy(woven[:, :VECTOR_END, t], page[t][:, :VECTOR_END])
                for c0, n in CHUNKS[1:]:
                    nc.scalar.copy(woven[:, c0 : c0 + n, t], page[t][:, c0 : c0 + n])

        out_scales = sb("out_scales", [P, U], U8)
        words_out = out_1[0].rearrange("p n t -> p (n t)").bitcast(I32)
        for i, (c0, n) in enumerate(CHUNKS):
            out_codes = sb("out_codes%d" % i, [P, n], U32)
            nc.vector.quantize_mx(
                out=out_codes[:].bitcast(FP8X4),
                scales=out_scales[:, c0 : c0 + n],
                in_=woven[:, c0 : c0 + n, :].rearrange("p c t -> p (c t)"),
            )
            nc.sync.dma_start(words_out[:, c0 : c0 + n], out_codes[:].bitcast(I32))
        for q in range(QUADS):
            queue = nc.sync if q < QUADS // 2 else nc.scalar
            queue.dma_start(out_2[0, 4 * q : 4 * q + 4, :].bitcast(I32), out_scales[32 * q : 32 * q + 4, :].bitcast(I32))
